import numpy as np
import ml_dtypes


def mxq(x, axis, fmt="e4m3"):
    dtype, down = {"e4m3": (ml_dtypes.float8_e4m3fn, 7), "e5m2": (ml_dtypes.float8_e5m2, 14)}[fmt]
    v = np.moveaxis(np.asarray(x, np.float32).astype(ml_dtypes.bfloat16).astype(np.float64), axis, -1)
    blocks = v.reshape(v.shape[:-1] + (-1, 32))
    amax = np.abs(blocks).max(-1, keepdims=True)
    byte = np.maximum(np.where(amax > 0, np.frexp(amax)[1] - 1 + 127, 0) - down, 1)
    scale = np.exp2(byte - 127.0)
    codes = (blocks / scale).astype(np.float32).astype(dtype).astype(np.float64)
    return np.moveaxis((codes * scale).reshape(v.shape), -1, axis)


WIDE = False


def mx_kscale(k):
    if not WIDE:
        return np.ones(k)
    levels = np.array([10, -10, 5, -5, 0])
    if k % 512:
        return np.exp2(np.random.permutation(np.resize(levels, k // 32))).repeat(32)
    a = np.empty((k // 512, 16))
    for p in range(k // 512):
        a[p, :8] = np.random.permutation(np.resize(levels, 8))
        for g in range(8):
            far = levels[np.abs(levels - a[p, g]) >= 10]
            a[p, g + 8] = far[np.random.randint(len(far))]
    return np.exp2(a.ravel()).repeat(32)


BF16 = ml_dtypes.bfloat16


def bf(x):
    return np.asarray(x, np.float32).astype(BF16)


def f64(x):
    return np.asarray(x).astype(np.float64)

def planes(Y):
    n, m = Y.shape
    b = f64(bf(Y)).reshape(n // 32, 32, m)
    amax = np.abs(b).max(1)
    byte = np.clip(np.where(amax > 0, np.frexp(amax)[1] - 1 + 127 - 7, 1), 1, 254)
    codes = (b * np.exp2(127.0 - byte)[:, None, :]).reshape(n, m).astype(np.float32).astype(ml_dtypes.float8_e4m3fn).view(np.uint8)
    words = codes.reshape(n // 512, 128, 4, m).transpose(0, 1, 3, 2)
    return np.ascontiguousarray(words), np.ascontiguousarray(byte.astype(np.uint8).reshape(n // 512, 16, m))


N, G, C = 256, 6, 512

GC = G * C

K = (
    (0, 1, 2, 3, 4, 5),
    (2, 0, 1, 5, 3, 4),
    (1, 2, 0, 4, 5, 3),
    (3, 5, 4, 0, 2, 1),
    (4, 3, 5, 1, 0, 2),
    (5, 4, 3, 2, 1, 0),
)


def setup_inputs():
    s = mx_kscale(C)
    t = mx_kscale(C)
    x = np.random.standard_normal((N, G, C)) * s[None, None, :]
    w1 = np.random.standard_normal((G, C, C)) / np.sqrt(GC) / s[None, :, None]
    b1 = 0.4 * np.random.standard_normal(C)
    ls = (1.0 + 0.1 * np.random.standard_normal(C)) * t
    w2 = np.random.standard_normal((G, C, C)) / np.sqrt(GC) / t[None, :, None]
    return {"x": bf(x), "w1": bf(w1), "b1": bf(b1), "ls": bf(ls), "w2": bf(w2)}


def sigmoid(v):
    return 1.0 / (1.0 + np.exp(-v))


def all_products(a, w):
    n, g, c = a.shape
    j, _, d = w.shape
    rows = np.reshape(a, (n * g, c))
    cols = np.reshape(np.transpose(w, (1, 0, 2)), (c, j * d))
    return np.reshape(mxq(rows, 1, "e4m3") @ mxq(cols, 0, "e4m3"), (n, g, j, d))


def gather_sum(p, g):
    total = p[:, 0, K[0][g], :]
    for h in range(1, G):
        total = total + p[:, h, K[h][g], :]
    return total


def group_combine(p):
    return np.stack([gather_sum(p, g) for g in range(G)], axis=1)


def core(x, w1, b1, ls, w2):
    p = all_products(f64(x), f64(w1))
    y = group_combine(p) + f64(b1)[None, None, :]

    m = np.max(y, axis=1)
    e = y * sigmoid(m)[:, None, :] * f64(ls)[None, None, :]

    q = all_products(e, f64(w2))
    z = group_combine(q)
    return z


def reference(x, w1, b1, ls, w2):
    R_out = core(x, w1, b1, ls, w2)
    words, scales = planes(np.moveaxis(R_out, 2, 0).reshape(512, -1))
    return R_out, words, scales

@@ -1,0 +1,465 @@
+from contextlib import ExitStack
+
+import concourse.mybir as mybir
+from concourse.masks import make_identity
+
+F32 = mybir.dt.float32
+BF16 = mybir.dt.bfloat16
+U32 = mybir.dt.uint32
+I32 = mybir.dt.int32
+U8 = mybir.dt.uint8
+FP8X4 = mybir.dt.float8_e4m3fn_x4
+ACT = mybir.ActivationFunctionType
+ALU = mybir.AluOpType
+
+N, G, C = 256, 6, 512
+FLOPS = 2 * (2 * N * G * G * C * C)
+
+K = (
+    (0, 1, 2, 3, 4, 5),
+    (2, 0, 1, 5, 3, 4),
+    (1, 2, 0, 4, 5, 3),
+    (3, 5, 4, 0, 2, 1),
+    (4, 3, 5, 1, 0, 2),
+    (5, 4, 3, 2, 1, 0),
+)
+PAIRS = ((0, 3), (1, 5), (2, 4))
+P = 128
+SLOTS = 4
+
+
+def source(pair, j):
+    a, b = PAIRS[pair]
+    h = [k for k in range(G) if K[k][a] == j][0]
+    h2 = [k for k in range(G) if K[k][b] == j][0]
+    for q, (c, e) in enumerate(PAIRS):
+        if (h, h2) == (c, e):
+            return q, 0
+        if (h, h2) == (e, c):
+            return q, 1
+    raise ValueError("not a pair")
+
+
+def place(h):
+    for q, pr in enumerate(PAIRS):
+        if h in pr:
+            return q, pr.index(h)
+    raise ValueError("no such element")
+
+
+def tile_dihedralthreegroupblock_x1_kernel(tc, x, w1, b1, ls, w2, out, out_words, out_scales):
+    nc = tc.nc
+    with ExitStack() as ctx:
+        const = ctx.enter_context(tc.tile_pool(name="const", bufs=1))
+        stage = ctx.enter_context(tc.tile_pool(name="stage", bufs=1))
+        psum = ctx.enter_context(tc.psum_pool(name="psum", bufs=1))
+
+        def sb(shape, dtype, name, bufs=1):
+            return stage.tile(shape, dtype, name=name, bufs=bufs, align_bytes=64)
+
+        def bank(i):
+            return psum.tile([P, 512], F32, name="bank%d" % i)
+
+        ident = const.tile([P, P], F32, name="ident", align_bytes=64)
+        make_identity(nc, ident[:])
+        b1_raw = const.tile([P, SLOTS], BF16, name="b1_raw")
+        ls_raw = const.tile([P, SLOTS], BF16, name="ls_raw")
+        b1_col = const.tile([P, SLOTS], F32, name="b1_col")
+        ls_col = const.tile([P, SLOTS], F32, name="ls_col")
+        warm = const.tile([P, 2], F32, name="warm")
+
+        x_raw = [sb([P, G, C], BF16, "x_raw%d" % b) for b in range(2)]
+        w_raw = [[sb([P, 4, C], BF16, "w%d_raw%d" % (s, j)) for j in range(G)] for s in range(2)]
+        x_il = [sb([P, 3, 2, P, 4], BF16, "x_il%d" % b) for b in range(2)]
+        x_cod = [sb([P, 3, 3 * P], U32, "x_cod%d" % b) for b in range(2)]
+        x_sca = [sb([P, 3, 3 * P], U8, "x_sca%d" % b) for b in range(2)]
+        w_cod = [[sb([P, C], U32, "w%d_cod%d" % (s, j)) for j in range(G)] for s in range(2)]
+        w_sca = [[sb([P, C], U8, "w%d_sca%d" % (s, j)) for j in range(G)] for s in range(2)]
+        y = [sb([P, SLOTS, 3, 2, P], F32, "y%d" % b) for b in range(2)]
+        e_il = [sb([P, G, P, 4], BF16, "e_il%d" % b) for b in range(2)]
+        e_cod = [sb([P, G, P], U32, "e_cod%d" % b) for b in range(2)]
+        e_sca = [sb([P, G, P], U8, "e_sca%d" % b) for b in range(2)]
+        r_il = [sb([P, P, G, 4], BF16, "r_il%d" % b) for b in range(2)]
+        r_cod = [sb([P, P * G], U32, "r_cod%d" % b) for b in range(2)]
+        r_sca = [sb([P, P * G], U8, "r_sca%d" % b) for b in range(2)]
+        w_il = {}
+
+        def load_x(b, q):
+            lo, hi = PAIRS[q]
+            nc.sync.dma_start(out=x_raw[b][:, lo : hi + 1 : hi - lo, :], in_=x[b * P : (b + 1) * P, lo : hi + 1 : hi - lo, :])
+
+        def load_x_all(b):
+            nc.sync.dma_start(out=x_raw[b][:], in_=x[b * P : (b + 1) * P, :, :])
+
+        def load_w(s, j):
+            w = (w1, w2)[s]
+            nc.sync.dma_start(out=w_raw[s][j][:], in_=w[j].rearrange("(p t) d -> p t d", t=4))
+
+        x_bank = {}
+
+        def turn_x(b, q, i):
+            t = bank(i)
+            x_bank[b, q] = t
+            words = x_raw[b][:].rearrange("p g c -> p (g c)").bitcast(F32)
+            for m, h in enumerate(PAIRS[q]):
+                for u in range(2):
+                    nc.tensor.transpose(t[:, (2 * m + u) * P : (2 * m + u + 1) * P], words[:, 256 * h + u : 256 * (h + 1) : 2], ident[:])
+
+        def copy_x(b, q, eng):
+            src = x_bank[b, q][:].rearrange("p (m u n) -> p m n u", m=2, u=2)
+            dst = x_il[b][:, q].rearrange("p m n t -> p (m n t)").bitcast(F32).rearrange("p (m n u) -> p m n u", m=2, u=2)
+            if eng == "v":
+                nc.vector.tensor_copy(out=dst, in_=src)
+            else:
+                nc.scalar.copy(out=dst, in_=src)
+
+        def quant(cod, sca, src):
+            nc.vector.quantize_mx(out=cod.bitcast(FP8X4), scales=sca, in_=src)
+
+        def quant_x(b, q):
+            flat = x_il[b][:, q].rearrange("p m n t -> p (m n t)")
+            quant(x_cod[b][:, q, 0 : 2 * P], x_sca[b][:, q, 0 : 2 * P], flat)
+            quant(x_cod[b][:, q, 2 * P : 3 * P], x_sca[b][:, q, 2 * P : 3 * P], flat[:, 0 : 4 * P])
+
+        def il_w(s, j, lo, hi, eng):
+            if (s, j) not in w_il:
+                w_il[s, j] = sb([P, 4 * C], BF16, "w_il", bufs=4)
+            dst = w_il[s, j][:, lo * C : hi * C]
+            if s == 0:
+                d = dst.rearrange("p (t m k) -> p t m k", t=hi - lo, k=4)
+                v = w_raw[s][j][:].rearrange("p k (m t) -> p t m k", t=4)[:, lo:hi]
+            else:
+                d = dst.rearrange("p (c k) -> p c k", k=4)
+                v = w_raw[s][j][:].rearrange("p k c -> p c k")[:, lo * P : hi * P]
+            if eng == "v":
+                nc.vector.tensor_copy(out=d, in_=v)
+            else:
+                nc.scalar.copy(out=d, in_=v)
+
+        def quant_w(s, j, lo=0, hi=4):
+            quant(w_cod[s][j][:, lo * P : hi * P], w_sca[s][j][:, lo * P : hi * P], w_il[s, j][:, lo * C : hi * C])
+
+        def mm1(b, dst, slot, pair, j, start, stop):
+            q, turned = source(pair, j)
+            cols = slice(turned * P, turned * P + 2 * P)
+            sl = slice(slot * P, (slot + 1) * P)
+            nc.tensor.matmul_mx(
+                out=dst,
+                lhsT=w_cod[0][j][:, sl].bitcast(FP8X4),
+                lhsT_scale=w_sca[0][j][:, sl],
+                rhs=x_cod[b][:, q, cols].bitcast(FP8X4),
+                rhs_scale=x_sca[b][:, q, cols],
+                start=start,
+                stop=stop,
+            )
+
+        def group1(b, dst, slot, pair):
+            for i in range(G):
+                mm1(b, dst, slot, pair, i, i == 0, i == G - 1)
+
+        def evac1(b, slot, src, lo, hi, step=1, eng="s"):
+            o = y[b][:, slot, lo:hi:step].rearrange("p q m n -> p q (m n)")
+            i = src.rearrange("p (q c) -> p q c", c=2 * P)
+            bias = b1_col[:, slot : slot + 1]
+            if eng == "v":
+                nc.vector.tensor_scalar(out=o, in0=i, scalar1=bias, scalar2=None, op0=ALU.add)
+            else:
+                nc.scalar.activation(out=o, in_=i, func=ACT.Identity, bias=bias)
+
+        gate = {}
+
+        def gate_max1(b, lo, hi):
+            if ("t1", b) not in gate:
+                gate["t1", b] = sb([P, SLOTS, 2, P], F32, "t1")
+                gate["t2", b] = sb([P, SLOTS, 2, P], F32, "t2")
+                gate["m", b] = sb([P, SLOTS, P], F32, "m")
+                gate["sg", b] = sb([P, SLOTS, P], F32, "sg")
+                gate["sp", b] = sb([P, SLOTS, P], F32, "sp")
+            nc.vector.tensor_tensor(out=gate["t1", b][:, lo:hi], in0=y[b][:, lo:hi, 0], in1=y[b][:, lo:hi, 1], op=ALU.max)
+
+        def gate_max2(b, lo, hi):
+            nc.vector.tensor_tensor(out=gate["t2", b][:, lo:hi], in0=gate["t1", b][:, lo:hi], in1=y[b][:, lo:hi, 2], op=ALU.max)
+
+        def gate_max3(b, lo, hi):
+            nc.vector.tensor_tensor(out=gate["m", b][:, lo:hi], in0=gate["t2", b][:, lo:hi, 0], in1=gate["t2", b][:, lo:hi, 1], op=ALU.max)
+
+        def gate_sig(b, lo, hi):
+            nc.scalar.activation(out=gate["sg", b][:, lo:hi], in_=gate["m", b][:, lo:hi], func=ACT.Sigmoid)
+            for s in range(lo, hi):
+                nc.scalar.activation(out=gate["sp", b][:, s], in_=gate["sg", b][:, s], func=ACT.Copy, scale=ls_col[:, s : s + 1])
+
+        def gate_mul(b, h):
+            q, m = place(h)
+            nc.vector.tensor_tensor(
+                out=e_il[b][:, h],
+                in0=y[b][:, :, q, m].rearrange("p s n -> p n s"),
+                in1=gate["sp", b][:].rearrange("p s n -> p n s"),
+                op=ALU.mult,
+            )
+
+        def quant_e(b, lo, hi):
+            quant(
+                e_cod[b][:, lo:hi].rearrange("p h n -> p (h n)"),
+                e_sca[b][:, lo:hi].rearrange("p h n -> p (h n)"),
+                e_il[b][:, lo:hi].rearrange("p h n t -> p (h n t)"),
+            )
+
+        def mm2(b, dst, g, j, start, stop):
+            h = [k for k in range(G) if K[k][g] == j][0]
+            nc.tensor.matmul_mx(
+                out=dst,
+                lhsT=e_cod[b][:, h].bitcast(FP8X4),
+                lhsT_scale=e_sca[b][:, h],
+                rhs=w_cod[1][j][:].bitcast(FP8X4),
+                rhs_scale=w_sca[1][j][:],
+                start=start,
+                stop=stop,
+            )
+
+        res = {}
+
+        def evac2(b, g, src):
+            o = sb([P, C], F32, "o32", bufs=8)
+            nc.scalar.copy(out=o[:], in_=src)
+            nc.sync.dma_start(out=out[b * P : (b + 1) * P, g, :], in_=o[:])
+            res["o", b, g] = o
+
+        def cast2(b, g):
+            o = sb([P, C], BF16, "obf", bufs=4)
+            nc.vector.tensor_copy(
+                out=o[:].rearrange("p (u w e) -> p u w e", u=2, e=2),
+                in_=res["o", b, g][:].rearrange("p (w u e) -> p u w e", u=2, e=2),
+            )
+            res["b", b, g] = o
+
+        def turn2(b, g, dst):
+            words = res["b", b, g][:].bitcast(F32)
+            for u in range(2):
+                i = 2 * (g % 2) + u
+                nc.tensor.transpose(dst[:, i * P : (i + 1) * P], words[:, u * P : (u + 1) * P], ident[:])
+
+        def copy2(b, q, src, eng):
+            d = r_il[b][:].rearrange("p n g t -> p (n g t)").bitcast(F32).rearrange("p (n q i) -> p n q i", q=3, i=4)[:, :, q]
+            v = src[:].rearrange("p (i n) -> p n i", i=4)
+            if eng == "v":
+                nc.vector.tensor_copy(out=d, in_=v)
+            else:
+                nc.scalar.copy(out=d, in_=v)
+
+        def quant_r(b, lo, hi):
+            flat = r_il[b][:].rearrange("p n g t -> p (n g t)")
+            quant(r_cod[b][:, lo:hi], r_sca[b][:, lo:hi], flat[:, 4 * lo : 4 * hi])
+
+        def store_r(b):
+            cols = slice(b * P * G, (b + 1) * P * G)
+            nc.sync.dma_start(
+                out=out_words[0, :, cols, :].rearrange("p m t -> p (m t)").bitcast(I32),
+                in_=r_cod[b][:].bitcast(I32),
+            )
+            for k in range(4):
+                nc.sync.dma_start(
+                    out=out_scales[0, 4 * k : 4 * k + 4, cols].bitcast(I32),
+                    in_=r_sca[b][32 * k : 32 * k + 4, :].bitcast(I32),
+                )
+
+        with tc.manual_schedule():
+            nc.vector.memset(warm[:], 0.0)
+            nc.scalar.activation(out=warm[:], in_=warm[:], func=ACT.Sigmoid)
+            nc.gpsimd.dma_start(out=b1_raw[:], in_=b1.rearrange("(p t) -> p t", t=4))
+            nc.gpsimd.dma_start(out=ls_raw[:], in_=ls.rearrange("(p t) -> p t", t=4))
+            nc.gpsimd.tensor_copy(out=b1_col[:], in_=b1_raw[:])
+            nc.gpsimd.tensor_copy(out=ls_col[:], in_=ls_raw[:])
+            load_w(0, 0)
+            for q in range(3):
+                load_x(0, q)
+            for j in range(1, G):
+                load_w(0, j)
+            load_w(1, 0)
+            load_x_all(1)
+            for j in range(1, G):
+                load_w(1, j)
+
+            for q in range(3):
+                turn_x(0, q, q)
+            il_w(0, 0, 0, 3, "v")
+            il_w(0, 0, 3, 4, "s")
+            quant_w(0, 0)
+            copy_x(0, 0, "s")
+            copy_x(0, 1, "s")
+            copy_x(0, 2, "s")
+            il_w(0, 1, 2, 4, "s")
+            quant_x(0, 0)
+            quant_x(0, 1)
+            il_w(0, 1, 0, 2, "v")
+            quant_w(0, 1, 0, 2)
+            quant_x(0, 2)
+            for j in range(2, G):
+                il_w(0, j, 0, 2, "v")
+                il_w(0, j, 2, 4, "s")
+                quant_w(0, j - 1, 2, 4)
+                quant_w(0, j, 0, 2)
+            quant_w(0, G - 1, 2, 4)
+
+            acc = {}
+            order = (6, 7, 0, 1, 2, 3, 4, 5)
+            for i in range(8):
+                acc[i // 2, i % 2] = bank(order[i])
+            for j in range(G):
+                for slot in range(SLOTS):
+                    for pair in range(2):
+                        mm1(0, acc[slot, pair][:, 0 : 2 * P], slot, pair, j, j == 0, j == G - 1)
+
+            def w2_v(j, lo, hi):
+                il_w(1, j, lo, hi, "v")
+
+            def w2_s(j, lo, hi):
+                il_w(1, j, lo, hi, "s")
+
+            def conv_q2(slot):
+                group1(0, acc[slot, 0][:, 2 * P : 4 * P], slot, 2)
+
+            def evac_q1(slot, eng):
+                evac1(0, slot, acc[slot, 1][:, 0 : 2 * P], 1, 2, 1, eng)
+
+            def evac_q02(slot):
+                evac1(0, slot, acc[slot, 0][:], 0, 3, 2)
+
+            bk = {}
+            def conv_b(i, banks):
+                for slot in (2 * i, 2 * i + 1):
+                    bk[slot] = bank(banks[slot % 2])
+                    group1(1, bk[slot][:, 0 : 2 * P], slot, 0)
+                    group1(1, bk[slot][:, 2 * P : 4 * P], slot, 1)
+                bk["z", i] = bank(banks[2])
+                for k in range(2):
+                    group1(1, bk["z", i][:, 2 * P * k : 2 * P * (k + 1)], 2 * i + k, 2)
+            def evac_b(slot):
+                evac1(1, slot, bk[slot][:], 0, 2)
+            def evac_z(i):
+                for k in range(2):
+                    evac1(1, 2 * i + k, bk["z", i][:, 2 * P * k : 2 * P * (k + 1)], 2, 3)
+            w2_s(0, 2, 4)
+            w2_v(0, 0, 2)
+            quant_w(1, 0)
+            evac_q1(0, "s")
+            evac_q1(1, "v")
+            evac_q1(2, "s")
+            evac_q1(3, "v")
+            conv_q2(0)
+            for q, i in enumerate((7, 1, 3)):
+                turn_x(1, q, i)
+            for slot in range(1, SLOTS):
+                conv_q2(slot)
+            evac_q02(0)
+            w2_v(1, 0, 2)
+            w2_s(1, 2, 3)
+            copy_x(1, 0, "v")
+            copy_x(1, 1, "s")
+            w2_v(2, 0, 1)
+            copy_x(1, 2, "v")
+            w2_s(1, 3, 4)
+            quant_x(1, 0)
+            quant_x(1, 1)
+            evac_q02(1)
+            gate_max1(0, 0, 2)
+            quant_x(1, 2)
+            gate_max2(0, 0, 2)
+            w2_s(2, 1, 3)
+            quant_w(1, 1)
+            gate_max3(0, 0, 2)
+            evac_q02(2)
+            evac_q02(3)
+            w2_s(2, 3, 4)
+            w2_v(3, 0, 1)
+            gate_max1(0, 2, 4)
+            w2_v(4, 0, 1)
+            gate_max2(0, 2, 4)
+            w2_s(3, 1, 4)
+            quant_w(1, 2)
+            gate_max3(0, 2, 4)
+            gate_sig(0, 0, 4)
+            w2_v(5, 0, 1)
+            quant_w(1, 3)
+            conv_b(0, (5, 6, 0))
+            conv_b(1, (7, 1, 3))
+            evac_b(0)
+            for h in range(4):
+                gate_mul(0, h)
+            evac_b(1)
+            gate_max1(1, 0, 2)
+            quant_e(0, 0, 4)
+            for h in range(4, 6):
+                gate_mul(0, h)
+            evac_z(0)
+            w2_s(4, 1, 4)
+            gate_max2(1, 0, 2)
+            quant_e(0, 4, 6)
+            gate_max3(1, 0, 2)
+            evac_b(2)
+            evac_b(3)
+            quant_w(1, 4)
+            gate_max1(1, 2, 4)
+            w2_s(5, 1, 2)
+            evac_z(1)
+            w2_s(5, 2, 4)
+            gate_max2(1, 2, 4)
+            gate_max3(1, 2, 4)
+            gate_sig(1, 0, 4)
+            quant_w(1, 5)
+            for h in range(6):
+                gate_mul(1, h)
+            quant_e(1, 0, 4)
+            quant_e(1, 4, 6)
+
+            group_bank = (2, 4, 5, 6, 0, 7)
+            turn_bank = (1, 3)
+            count = [0]
+
+            def turns(b, q):
+                t = bank(turn_bank[count[0] % 2])
+                count[0] += 1
+                turn2(b, 2 * q, t)
+                turn2(b, 2 * q + 1, t)
+                return t
+
+            acc2 = [bank(group_bank[g]) for g in range(G)]
+            for j in range(4):
+                for g in range(G):
+                    mm2(0, acc2[g][:], g, j, j == 0, False)
+            for g in range(G):
+                for j in range(4, G):
+                    mm2(0, acc2[g][:], g, j, False, j == G - 1)
+                evac2(0, g, acc2[g][:])
+                cast2(0, g)
+
+            def conv2(b, g):
+                t = bank(group_bank[g])
+                for j in range(G):
+                    mm2(b, t[:], g, j, j == 0, j == G - 1)
+                evac2(b, g, t[:])
+                cast2(b, g)
+
+            conv2(1, 0)
+            conv2(1, 1)
+            t = turns(0, 0)
+            s = turns(0, 1)
+            copy2(0, 0, t, "v")
+            copy2(0, 1, s, "v")
+            conv2(1, 2)
+            conv2(1, 3)
+            t = turns(0, 2)
+            s = turns(1, 0)
+            copy2(0, 2, t, "v")
+            copy2(1, 0, s, "v")
+            quant_r(0, 0, 512)
+            quant_r(0, 512, 768)
+            store_r(0)
+            conv2(1, 4)
+            conv2(1, 5)
+            t = turns(1, 1)
+            s = turns(1, 2)
+            copy2(1, 1, t, "v")
+            copy2(1, 2, s, "v")
+            quant_r(1, 0, 512)
+            quant_r(1, 512, 768)
+            store_r(1)

@@ -67,6 +67,7 @@ def tile_dihedralthreegroupblock_x1_kernel(tc, x, w1, b1, ls, w2, out, out_words
         b1_col = const.tile([P, SLOTS], F32, name="b1_col")
         ls_col = const.tile([P, SLOTS], F32, name="ls_col")
         warm = const.tile([P, 2], F32, name="warm")
+        zeros = const.tile([P, C], BF16, name="zeros", align_bytes=64)
 
         x_raw = [sb([P, G, C], BF16, "x_raw%d" % b) for b in range(2)]
         w_raw = [[sb([P, 4, C], BF16, "w%d_raw%d" % (s, j)) for j in range(G)] for s in range(2)]
@@ -224,11 +225,12 @@ def tile_dihedralthreegroupblock_x1_kernel(tc, x, w1, b1, ls, w2, out, out_words
             nc.sync.dma_start(out=out[b * P : (b + 1) * P, g, :], in_=o[:])
             res["o", b, g] = o
 
-        def cast2(b, g):
+        def cast2(b, g, src=None):
+            src = res["o", b, g][:] if src is None else src
             o = sb([P, C], BF16, "obf", bufs=4)
             nc.vector.tensor_copy(
                 out=o[:].rearrange("p (u w e) -> p u w e", u=2, e=2),
-                in_=res["o", b, g][:].rearrange("p (w u e) -> p u w e", u=2, e=2),
+                in_=src.rearrange("p (w u e) -> p u w e", u=2, e=2),
             )
             res["b", b, g] = o
 
@@ -238,9 +240,9 @@ def tile_dihedralthreegroupblock_x1_kernel(tc, x, w1, b1, ls, w2, out, out_words
                 i = 2 * (g % 2) + u
                 nc.tensor.transpose(dst[:, i * P : (i + 1) * P], words[:, u * P : (u + 1) * P], ident[:])
 
-        def copy2(b, q, src, eng):
-            d = r_il[b][:].rearrange("p n g t -> p (n g t)").bitcast(F32).rearrange("p (n q i) -> p n q i", q=3, i=4)[:, :, q]
-            v = src[:].rearrange("p (i n) -> p n i", i=4)
+        def copy2(b, q, src, eng, lo=0, hi=P):
+            d = r_il[b][:].rearrange("p n g t -> p (n g t)").bitcast(F32).rearrange("p (n q i) -> p n q i", q=3, i=4)[:, lo:hi, q]
+            v = src[:].rearrange("p (i n) -> p n i", i=4)[:, lo:hi]
             if eng == "v":
                 nc.vector.tensor_copy(out=d, in_=v)
             else:
@@ -250,14 +252,16 @@ def tile_dihedralthreegroupblock_x1_kernel(tc, x, w1, b1, ls, w2, out, out_words
             flat = r_il[b][:].rearrange("p n g t -> p (n g t)")
             quant(r_cod[b][:, lo:hi], r_sca[b][:, lo:hi], flat[:, 4 * lo : 4 * hi])
 
-        def store_r(b):
-            cols = slice(b * P * G, (b + 1) * P * G)
+        def store_words(b, lo, hi):
             nc.sync.dma_start(
-                out=out_words[0, :, cols, :].rearrange("p m t -> p (m t)").bitcast(I32),
-                in_=r_cod[b][:].bitcast(I32),
+                out=out_words[0, :, b * P * G + lo : b * P * G + hi, :].rearrange("p m t -> p (m t)").bitcast(I32),
+                in_=r_cod[b][:, lo:hi].bitcast(I32),
             )
+
+        def store_scales(b, eng):
+            cols = slice(b * P * G, (b + 1) * P * G)
             for k in range(4):
-                nc.sync.dma_start(
+                eng.dma_start(
                     out=out_scales[0, 4 * k : 4 * k + 4, cols].bitcast(I32),
                     in_=r_sca[b][32 * k : 32 * k + 4, :].bitcast(I32),
                 )
@@ -265,10 +269,14 @@ def tile_dihedralthreegroupblock_x1_kernel(tc, x, w1, b1, ls, w2, out, out_words
         with tc.manual_schedule():
             nc.vector.memset(warm[:], 0.0)
             nc.scalar.activation(out=warm[:], in_=warm[:], func=ACT.Sigmoid)
-            nc.gpsimd.dma_start(out=b1_raw[:], in_=b1.rearrange("(p t) -> p t", t=4))
-            nc.gpsimd.dma_start(out=ls_raw[:], in_=ls.rearrange("(p t) -> p t", t=4))
-            nc.gpsimd.tensor_copy(out=b1_col[:], in_=b1_raw[:])
-            nc.gpsimd.tensor_copy(out=ls_col[:], in_=ls_raw[:])
+            nc.vector.memset(zeros[:], 0.0)
+            nc.scalar.dma_start(out=b1_raw[:], in_=b1.rearrange("(p t) -> p t", t=4))
+            nc.scalar.dma_start(out=ls_raw[:], in_=ls.rearrange("(p t) -> p t", t=4))
+            cold = bank(7)
+            for i in range(7):
+                nc.tensor.matmul(cold[:], lhsT=zeros[:, 0:P], rhs=zeros[:], start=True, stop=True)
+            nc.scalar.copy(out=b1_col[:], in_=b1_raw[:])
+            nc.scalar.copy(out=ls_col[:], in_=ls_raw[:])
             load_w(0, 0)
             for q in range(3):
                 load_x(0, q)
@@ -363,50 +371,56 @@ def tile_dihedralthreegroupblock_x1_kernel(tc, x, w1, b1, ls, w2, out, out_words
             evac_q02(1)
             gate_max1(0, 0, 2)
             quant_x(1, 2)
+            evac_q02(2)
             gate_max2(0, 0, 2)
-            w2_s(2, 1, 3)
+            w2_s(2, 1, 2)
             quant_w(1, 1)
             gate_max3(0, 0, 2)
-            evac_q02(2)
             evac_q02(3)
-            w2_s(2, 3, 4)
             w2_v(3, 0, 1)
             gate_max1(0, 2, 4)
+            gate_sig(0, 0, 2)
             w2_v(4, 0, 1)
             gate_max2(0, 2, 4)
-            w2_s(3, 1, 4)
-            quant_w(1, 2)
-            gate_max3(0, 2, 4)
-            gate_sig(0, 0, 4)
+            w2_s(2, 2, 4)
             w2_v(5, 0, 1)
-            quant_w(1, 3)
+            gate_max3(0, 2, 4)
+            gate_sig(0, 2, 4)
+            quant_w(1, 2)
             conv_b(0, (5, 6, 0))
             conv_b(1, (7, 1, 3))
+            w2_s(3, 1, 2)
             evac_b(0)
             for h in range(4):
                 gate_mul(0, h)
             evac_b(1)
-            gate_max1(1, 0, 2)
+            w2_s(3, 2, 4)
             quant_e(0, 0, 4)
             for h in range(4, 6):
                 gate_mul(0, h)
             evac_z(0)
-            w2_s(4, 1, 4)
-            gate_max2(1, 0, 2)
+            gate_max1(1, 0, 2)
             quant_e(0, 4, 6)
-            gate_max3(1, 0, 2)
+            w2_s(4, 1, 2)
+            gate_max2(1, 0, 2)
+            quant_w(1, 3)
             evac_b(2)
+            gate_max3(1, 0, 2)
+            w2_s(4, 2, 4)
             evac_b(3)
+            gate_sig(1, 0, 2)
             quant_w(1, 4)
             gate_max1(1, 2, 4)
-            w2_s(5, 1, 2)
             evac_z(1)
-            w2_s(5, 2, 4)
+            w2_s(5, 1, 3)
             gate_max2(1, 2, 4)
             gate_max3(1, 2, 4)
-            gate_sig(1, 0, 4)
+            gate_sig(1, 2, 4)
+            w2_s(5, 3, 4)
+            for h in range(3):
+                gate_mul(1, h)
             quant_w(1, 5)
-            for h in range(6):
+            for h in range(3, 6):
                 gate_mul(1, h)
             quant_e(1, 0, 4)
             quant_e(1, 4, 6)
@@ -453,13 +467,23 @@ def tile_dihedralthreegroupblock_x1_kernel(tc, x, w1, b1, ls, w2, out, out_words
             copy2(1, 0, s, "v")
             quant_r(0, 0, 512)
             quant_r(0, 512, 768)
-            store_r(0)
+            store_words(0, 0, 768)
+            store_scales(0, nc.sync)
             conv2(1, 4)
-            conv2(1, 5)
+            last = bank(group_bank[5])
+            for j in range(G):
+                mm2(1, last[:], 5, j, j == 0, j == G - 1)
+            cast2(1, 5, last[:])
             t = turns(1, 1)
             s = turns(1, 2)
-            copy2(1, 1, t, "v")
-            copy2(1, 2, s, "v")
-            quant_r(1, 0, 512)
-            quant_r(1, 512, 768)
-            store_r(1)
+            copy2(1, 1, t, "s")
+            evac2(1, 5, last[:])
+            copy2(1, 2, s, "v", 0, 64)
+            copy2(1, 2, s, "v", 64, P)
+            quant_r(1, 0, 256)
+            quant_r(1, 256, 384)
+            store_words(1, 0, 384)
+            quant_r(1, 384, 640)
+            quant_r(1, 640, 768)
+            store_words(1, 384, 768)
+            store_scales(1, nc.scalar)

@@ -24,6 +24,7 @@ K = (
     (5, 4, 3, 2, 1, 0),
 )
 PAIRS = ((0, 3), (1, 5), (2, 4))
+JO = (0, 5, 1, 2, 3, 4)
 P = 128
 SLOTS = 4
 
@@ -38,6 +39,10 @@ def source(pair, j):
         if (h, h2) == (e, c):
             return q, 1
     raise ValueError("not a pair")
+
+
+def element(j, g):
+    return [h for h in range(G) if K[h][g] == j][0]
 
 
 def place(h):
@@ -71,12 +76,18 @@ def tile_dihedralthreegroupblock_x1_kernel(tc, x, w1, b1, ls, w2, out, out_words
 
         x_raw = [sb([P, G, C], BF16, "x_raw%d" % b) for b in range(2)]
         w_raw = [[sb([P, 4, C], BF16, "w%d_raw%d" % (s, j)) for j in range(G)] for s in range(2)]
-        x_il = [sb([P, 3, 2, P, 4], BF16, "x_il%d" % b) for b in range(2)]
-        x_cod = [sb([P, 3, 3 * P], U32, "x_cod%d" % b) for b in range(2)]
-        x_sca = [sb([P, 3, 3 * P], U8, "x_sca%d" % b) for b in range(2)]
+        x_il = [sb([P, 2, N, 4], BF16, "x_il%d" % q) for q in range(3)]
+        x_cod = [sb([P, 3 * N], U32, "x_cod%d" % q) for q in range(3)]
+        x_sca = [sb([P, 3 * N], U8, "x_sca%d" % q) for q in range(3)]
         w_cod = [[sb([P, C], U32, "w%d_cod%d" % (s, j)) for j in range(G)] for s in range(2)]
         w_sca = [[sb([P, C], U8, "w%d_sca%d" % (s, j)) for j in range(G)] for s in range(2)]
-        y = [sb([P, SLOTS, 3, 2, P], F32, "y%d" % b) for b in range(2)]
+        y = sb([P, SLOTS, 3, 2, N], F32, "y")
+        t1 = sb([P, SLOTS, 2, N], F32, "t1")
+        t2 = [sb([P, SLOTS, 2, P], F32, "t2"), None]
+        t2[1] = t2[0]
+        top = [sb([P, SLOTS, P], F32, "top%d" % b) for b in range(2)]
+        sig = [sb([P, SLOTS, P], F32, "sig%d" % b) for b in range(2)]
+        fac = [sb([P, SLOTS, P], F32, "fac%d" % b) for b in range(2)]
         e_il = [sb([P, G, P, 4], BF16, "e_il%d" % b) for b in range(2)]
         e_cod = [sb([P, G, P], U32, "e_cod%d" % b) for b in range(2)]
         e_sca = [sb([P, G, P], U8, "e_sca%d" % b) for b in range(2)]
@@ -85,12 +96,12 @@ def tile_dihedralthreegroupblock_x1_kernel(tc, x, w1, b1, ls, w2, out, out_words
         r_sca = [sb([P, P * G], U8, "r_sca%d" % b) for b in range(2)]
         w_il = {}
 
+        def tok(b):
+            return slice(b * P, (b + 1) * P)
+
         def load_x(b, q):
             lo, hi = PAIRS[q]
-            nc.sync.dma_start(out=x_raw[b][:, lo : hi + 1 : hi - lo, :], in_=x[b * P : (b + 1) * P, lo : hi + 1 : hi - lo, :])
-
-        def load_x_all(b):
-            nc.sync.dma_start(out=x_raw[b][:], in_=x[b * P : (b + 1) * P, :, :])
+            nc.sync.dma_start(out=x_raw[b][:, lo : hi + 1 : hi - lo, :], in_=x[tok(b), lo : hi + 1 : hi - lo, :])
 
         def load_w(s, j):
             w = (w1, w2)[s]
@@ -98,8 +109,8 @@ def tile_dihedralthreegroupblock_x1_kernel(tc, x, w1, b1, ls, w2, out, out_words
 
         x_bank = {}
 
-        def turn_x(b, q, i):
-            t = bank(i)
+        def turn_x(b, q):
+            t = bank(2 * q + b)
             x_bank[b, q] = t
             words = x_raw[b][:].rearrange("p g c -> p (g c)").bitcast(F32)
             for m, h in enumerate(PAIRS[q]):
@@ -108,7 +119,7 @@ def tile_dihedralthreegroupblock_x1_kernel(tc, x, w1, b1, ls, w2, out, out_words
 
         def copy_x(b, q, eng):
             src = x_bank[b, q][:].rearrange("p (m u n) -> p m n u", m=2, u=2)
-            dst = x_il[b][:, q].rearrange("p m n t -> p (m n t)").bitcast(F32).rearrange("p (m n u) -> p m n u", m=2, u=2)
+            dst = x_il[q][:].rearrange("p m n t -> p (m n t)").bitcast(F32).rearrange("p (m n u) -> p m n u", m=2, u=2)[:, :, tok(b)]
             if eng == "v":
                 nc.vector.tensor_copy(out=dst, in_=src)
             else:
@@ -117,84 +128,88 @@ def tile_dihedralthreegroupblock_x1_kernel(tc, x, w1, b1, ls, w2, out, out_words
         def quant(cod, sca, src):
             nc.vector.quantize_mx(out=cod.bitcast(FP8X4), scales=sca, in_=src)
 
-        def quant_x(b, q):
-            flat = x_il[b][:, q].rearrange("p m n t -> p (m n t)")
-            quant(x_cod[b][:, q, 0 : 2 * P], x_sca[b][:, q, 0 : 2 * P], flat)
-            quant(x_cod[b][:, q, 2 * P : 3 * P], x_sca[b][:, q, 2 * P : 3 * P], flat[:, 0 : 4 * P])
+        def quant_x(q):
+            flat = x_il[q][:].rearrange("p m n t -> p (m n t)")
+            quant(x_cod[q][:, 0 : 2 * N], x_sca[q][:, 0 : 2 * N], flat)
+
+        def quant_x2(q):
+            flat = x_il[q][:].rearrange("p m n t -> p (m n t)")
+            quant(x_cod[q][:, 2 * N : 3 * N], x_sca[q][:, 2 * N : 3 * N], flat[:, 0 : 4 * N])
 
         def il_w(s, j, lo, hi, eng):
             if (s, j) not in w_il:
-                w_il[s, j] = sb([P, 4 * C], BF16, "w_il", bufs=4)
-            dst = w_il[s, j][:, lo * C : hi * C]
-            if s == 0:
-                d = dst.rearrange("p (t m k) -> p t m k", t=hi - lo, k=4)
-                v = w_raw[s][j][:].rearrange("p k (m t) -> p t m k", t=4)[:, lo:hi]
-            else:
-                d = dst.rearrange("p (c k) -> p c k", k=4)
-                v = w_raw[s][j][:].rearrange("p k c -> p c k")[:, lo * P : hi * P]
+                w_il[s, j] = sb([P, 4 * C], BF16, "w_il", bufs=3)
+            pat = ("p (t m k) -> p m k t", "p (m t k) -> p m k t")[s]
+            d = w_il[s, j][:].rearrange(pat, t=4, k=4)[:, lo * 32 : hi * 32]
+            v = w_raw[s][j][:].rearrange("p k (m t) -> p m k t", t=4)[:, lo * 32 : hi * 32]
             if eng == "v":
                 nc.vector.tensor_copy(out=d, in_=v)
             else:
                 nc.scalar.copy(out=d, in_=v)
 
+        def w1_v(j, lo, hi):
+            il_w(0, j, lo, hi, "v")
+
+        def w1_s(j, lo, hi):
+            il_w(0, j, lo, hi, "s")
+
+        def w2_v(j, lo, hi):
+            il_w(1, j, lo, hi, "v")
+
+        def w2_s(j, lo, hi):
+            il_w(1, j, lo, hi, "s")
+
         def quant_w(s, j, lo=0, hi=4):
             quant(w_cod[s][j][:, lo * P : hi * P], w_sca[s][j][:, lo * P : hi * P], w_il[s, j][:, lo * C : hi * C])
 
-        def mm1(b, dst, slot, pair, j, start, stop):
-            q, turned = source(pair, j)
-            cols = slice(turned * P, turned * P + 2 * P)
+        def mm1(dst, slot, j, q, cols, start, stop):
             sl = slice(slot * P, (slot + 1) * P)
             nc.tensor.matmul_mx(
                 out=dst,
                 lhsT=w_cod[0][j][:, sl].bitcast(FP8X4),
                 lhsT_scale=w_sca[0][j][:, sl],
-                rhs=x_cod[b][:, q, cols].bitcast(FP8X4),
-                rhs_scale=x_sca[b][:, q, cols],
+                rhs=x_cod[q][:, cols].bitcast(FP8X4),
+                rhs_scale=x_sca[q][:, cols],
                 start=start,
                 stop=stop,
             )
 
-        def group1(b, dst, slot, pair):
-            for i in range(G):
-                mm1(b, dst, slot, pair, i, i == 0, i == G - 1)
+        def pair_pass(dst, slot, pair, j, start, stop):
+            q, turned = source(pair, j)
+            mm1(dst, slot, j, q, slice(turned * N, turned * N + 2 * N), start, stop)
 
-        def evac1(b, slot, src, lo, hi, step=1, eng="s"):
-            o = y[b][:, slot, lo:hi:step].rearrange("p q m n -> p q (m n)")
-            i = src.rearrange("p (q c) -> p q c", c=2 * P)
+        def single_group(dst, slot, g, b):
+            for j in range(G):
+                q, m = place(element(j, g))
+                mm1(dst, slot, j, q, slice(m * N + b * P, m * N + (b + 1) * P), j == 0, j == G - 1)
+
+        def evac1(dst, src, slot, eng):
             bias = b1_col[:, slot : slot + 1]
             if eng == "v":
-                nc.vector.tensor_scalar(out=o, in0=i, scalar1=bias, scalar2=None, op0=ALU.add)
+                nc.vector.tensor_scalar(out=dst, in0=src, scalar1=bias, scalar2=None, op0=ALU.add)
             else:
-                nc.scalar.activation(out=o, in_=i, func=ACT.Identity, bias=bias)
+                nc.scalar.activation(out=dst, in_=src, func=ACT.Identity, bias=bias)
 
-        gate = {}
+        def max1(lo, hi):
+            nc.vector.tensor_tensor(out=t1[:, lo:hi], in0=y[:, lo:hi, 0], in1=y[:, lo:hi, 1], op=ALU.max)
 
-        def gate_max1(b, lo, hi):
-            if ("t1", b) not in gate:
-                gate["t1", b] = sb([P, SLOTS, 2, P], F32, "t1")
-                gate["t2", b] = sb([P, SLOTS, 2, P], F32, "t2")
-                gate["m", b] = sb([P, SLOTS, P], F32, "m")
-                gate["sg", b] = sb([P, SLOTS, P], F32, "sg")
-                gate["sp", b] = sb([P, SLOTS, P], F32, "sp")
-            nc.vector.tensor_tensor(out=gate["t1", b][:, lo:hi], in0=y[b][:, lo:hi, 0], in1=y[b][:, lo:hi, 1], op=ALU.max)
+        def max2(b, lo, hi):
+            nc.vector.tensor_tensor(out=t2[b][:, lo:hi], in0=t1[:, lo:hi, :, tok(b)], in1=y[:, lo:hi, 2, :, tok(b)], op=ALU.max)
 
-        def gate_max2(b, lo, hi):
-            nc.vector.tensor_tensor(out=gate["t2", b][:, lo:hi], in0=gate["t1", b][:, lo:hi], in1=y[b][:, lo:hi, 2], op=ALU.max)
-
-        def gate_max3(b, lo, hi):
-            nc.vector.tensor_tensor(out=gate["m", b][:, lo:hi], in0=gate["t2", b][:, lo:hi, 0], in1=gate["t2", b][:, lo:hi, 1], op=ALU.max)
+        def max3(b, lo, hi):
+            nc.vector.tensor_tensor(out=top[b][:, lo:hi], in0=t2[b][:, lo:hi, 0], in1=t2[b][:, lo:hi, 1], op=ALU.max)
 
         def gate_sig(b, lo, hi):
-            nc.scalar.activation(out=gate["sg", b][:, lo:hi], in_=gate["m", b][:, lo:hi], func=ACT.Sigmoid)
+            nc.scalar.activation(out=sig[b][:, lo:hi], in_=top[b][:, lo:hi], func=ACT.Sigmoid)
             for s in range(lo, hi):
-                nc.scalar.activation(out=gate["sp", b][:, s], in_=gate["sg", b][:, s], func=ACT.Copy, scale=ls_col[:, s : s + 1])
+                nc.scalar.activation(out=fac[b][:, s], in_=sig[b][:, s], func=ACT.Copy, scale=ls_col[:, s : s + 1])
 
         def gate_mul(b, h):
             q, m = place(h)
             nc.vector.tensor_tensor(
-                out=e_il[b][:, h],
-                in0=y[b][:, :, q, m].rearrange("p s n -> p n s"),
-                in1=gate["sp", b][:].rearrange("p s n -> p n s"),
+                out=e_il[b][:, h].rearrange("p (c i) s -> p c s i", i=4),
+                in0=y[:, :, q, m, tok(b)].rearrange("p s (c i) -> p c s i", i=4),
+                in1=fac[b][:].rearrange("p s (c i) -> p c s i", i=4),
                 op=ALU.mult,
             )
 
@@ -206,7 +221,7 @@ def tile_dihedralthreegroupblock_x1_kernel(tc, x, w1, b1, ls, w2, out, out_words
             )
 
         def mm2(b, dst, g, j, start, stop):
-            h = [k for k in range(G) if K[k][g] == j][0]
+            h = element(j, g)
             nc.tensor.matmul_mx(
                 out=dst,
                 lhsT=e_cod[b][:, h].bitcast(FP8X4),
@@ -219,15 +234,18 @@ def tile_dihedralthreegroupblock_x1_kernel(tc, x, w1, b1, ls, w2, out, out_words
 
         res = {}
 
-        def evac2(b, g, src):
-            o = sb([P, C], F32, "o32", bufs=8)
-            nc.scalar.copy(out=o[:], in_=src)
+        def evac2(b, g, src, eng="s"):
+            o = sb([P, C], F32, "o32", bufs=6)
+            if eng == "v":
+                nc.vector.tensor_copy(out=o[:], in_=src)
+            else:
+                nc.scalar.copy(out=o[:], in_=src)
             nc.sync.dma_start(out=out[b * P : (b + 1) * P, g, :], in_=o[:])
             res["o", b, g] = o
 
         def cast2(b, g, src=None):
             src = res["o", b, g][:] if src is None else src
-            o = sb([P, C], BF16, "obf", bufs=4)
+            o = sb([P, C], BF16, "obf", bufs=8)
             nc.vector.tensor_copy(
                 out=o[:].rearrange("p (u w e) -> p u w e", u=2, e=2),
                 in_=src.rearrange("p (w u e) -> p u w e", u=2, e=2),
@@ -273,160 +291,179 @@ def tile_dihedralthreegroupblock_x1_kernel(tc, x, w1, b1, ls, w2, out, out_words
             nc.scalar.dma_start(out=b1_raw[:], in_=b1.rearrange("(p t) -> p t", t=4))
             nc.scalar.dma_start(out=ls_raw[:], in_=ls.rearrange("(p t) -> p t", t=4))
             cold = bank(7)
-            for i in range(7):
-                nc.tensor.matmul(cold[:], lhsT=zeros[:, 0:P], rhs=zeros[:], start=True, stop=True)
+
+            def warm_up(n):
+                for i in range(n):
+                    nc.tensor.matmul(cold[:], lhsT=zeros[:, 0:P], rhs=zeros[:], start=True, stop=True)
+
+            warm_up(4)
             nc.scalar.copy(out=b1_col[:], in_=b1_raw[:])
             nc.scalar.copy(out=ls_col[:], in_=ls_raw[:])
-            load_w(0, 0)
-            for q in range(3):
-                load_x(0, q)
-            for j in range(1, G):
-                load_w(0, j)
-            load_w(1, 0)
-            load_x_all(1)
-            for j in range(1, G):
+            load_x(0, 0)
+            load_x(1, 0)
+            load_w(0, JO[0])
+            load_x(0, 1)
+            load_x(1, 1)
+            load_x(0, 2)
+            load_x(1, 2)
+            for i in range(1, G):
+                load_w(0, JO[i])
+            for j in range(G):
                 load_w(1, j)
-
-            for q in range(3):
-                turn_x(0, q, q)
-            il_w(0, 0, 0, 3, "v")
-            il_w(0, 0, 3, 4, "s")
-            quant_w(0, 0)
-            copy_x(0, 0, "s")
-            copy_x(0, 1, "s")
-            copy_x(0, 2, "s")
-            il_w(0, 1, 2, 4, "s")
-            quant_x(0, 0)
-            quant_x(0, 1)
-            il_w(0, 1, 0, 2, "v")
-            quant_w(0, 1, 0, 2)
-            quant_x(0, 2)
-            for j in range(2, G):
-                il_w(0, j, 0, 2, "v")
-                il_w(0, j, 2, 4, "s")
-                quant_w(0, j - 1, 2, 4)
-                quant_w(0, j, 0, 2)
-            quant_w(0, G - 1, 2, 4)
 
             acc = {}
             order = (6, 7, 0, 1, 2, 3, 4, 5)
-            for i in range(8):
-                acc[i // 2, i % 2] = bank(order[i])
-            for j in range(G):
+
+            def sweep(pair, i):
                 for slot in range(SLOTS):
-                    for pair in range(2):
-                        mm1(0, acc[slot, pair][:, 0 : 2 * P], slot, pair, j, j == 0, j == G - 1)
+                    if i == 0:
+                        acc[slot, pair] = bank(order[4 * pair + slot])
+                    pair_pass(acc[slot, pair][:], slot, pair, JO[i], i == 0, False)
 
-            def w2_v(j, lo, hi):
-                il_w(1, j, lo, hi, "v")
+            def finish(slot, pair):
+                for i in (4, 5):
+                    pair_pass(acc[slot, pair][:], slot, pair, JO[i], False, i == 5)
 
-            def w2_s(j, lo, hi):
-                il_w(1, j, lo, hi, "s")
+            def evac_p(slot, pair, eng):
+                evac1(y[:, slot, pair].rearrange("p m n -> p (m n)"), acc[slot, pair][:], slot, eng)
 
-            def conv_q2(slot):
-                group1(0, acc[slot, 0][:, 2 * P : 4 * P], slot, 2)
+            last = {}
+            def single(b, slot):
+                last[b, slot] = bank(order[4 * b + slot])
+                for m in range(2):
+                    single_group(last[b, slot][:, m * P : (m + 1) * P], slot, PAIRS[2][m], b)
 
-            def evac_q1(slot, eng):
-                evac1(0, slot, acc[slot, 1][:, 0 : 2 * P], 1, 2, 1, eng)
+            def evac_s(b, slot, eng):
+                evac1(y[:, slot, 2, :, tok(b)], last[b, slot][:, 0 : 2 * P].rearrange("p (m n) -> p m n", m=2), slot, eng)
 
-            def evac_q02(slot):
-                evac1(0, slot, acc[slot, 0][:], 0, 3, 2)
-
-            bk = {}
-            def conv_b(i, banks):
-                for slot in (2 * i, 2 * i + 1):
-                    bk[slot] = bank(banks[slot % 2])
-                    group1(1, bk[slot][:, 0 : 2 * P], slot, 0)
-                    group1(1, bk[slot][:, 2 * P : 4 * P], slot, 1)
-                bk["z", i] = bank(banks[2])
-                for k in range(2):
-                    group1(1, bk["z", i][:, 2 * P * k : 2 * P * (k + 1)], 2 * i + k, 2)
-            def evac_b(slot):
-                evac1(1, slot, bk[slot][:], 0, 2)
-            def evac_z(i):
-                for k in range(2):
-                    evac1(1, 2 * i + k, bk["z", i][:, 2 * P * k : 2 * P * (k + 1)], 2, 3)
-            w2_s(0, 2, 4)
-            w2_v(0, 0, 2)
-            quant_w(1, 0)
-            evac_q1(0, "s")
-            evac_q1(1, "v")
-            evac_q1(2, "s")
-            evac_q1(3, "v")
-            conv_q2(0)
-            for q, i in enumerate((7, 1, 3)):
-                turn_x(1, q, i)
-            for slot in range(1, SLOTS):
-                conv_q2(slot)
-            evac_q02(0)
-            w2_v(1, 0, 2)
-            w2_s(1, 2, 3)
-            copy_x(1, 0, "v")
+            turn_x(0, 0)
+            turn_x(1, 0)
+            copy_x(0, 0, "s")
+            copy_x(1, 0, "s")
+            w1_v(JO[0], 0, 3)
+            w1_s(JO[0], 3, 4)
+            warm_up(2)
+            turn_x(0, 1)
+            turn_x(1, 1)
+            warm_up(2)
+            quant_x(0)
+            quant_w(0, JO[0], 0, 2)
+            quant_w(0, JO[0], 2, 4)
+            copy_x(0, 1, "s")
             copy_x(1, 1, "s")
-            w2_v(2, 0, 1)
-            copy_x(1, 2, "v")
-            w2_s(1, 3, 4)
-            quant_x(1, 0)
-            quant_x(1, 1)
-            evac_q02(1)
-            gate_max1(0, 0, 2)
-            quant_x(1, 2)
-            evac_q02(2)
-            gate_max2(0, 0, 2)
-            w2_s(2, 1, 2)
-            quant_w(1, 1)
-            gate_max3(0, 0, 2)
-            evac_q02(3)
-            w2_v(3, 0, 1)
-            gate_max1(0, 2, 4)
-            gate_sig(0, 0, 2)
-            w2_v(4, 0, 1)
-            gate_max2(0, 2, 4)
-            w2_s(2, 2, 4)
-            w2_v(5, 0, 1)
-            gate_max3(0, 2, 4)
-            gate_sig(0, 2, 4)
-            quant_w(1, 2)
-            conv_b(0, (5, 6, 0))
-            conv_b(1, (7, 1, 3))
-            w2_s(3, 1, 2)
-            evac_b(0)
-            for h in range(4):
-                gate_mul(0, h)
-            evac_b(1)
-            w2_s(3, 2, 4)
-            quant_e(0, 0, 4)
-            for h in range(4, 6):
-                gate_mul(0, h)
-            evac_z(0)
-            gate_max1(1, 0, 2)
-            quant_e(0, 4, 6)
-            w2_s(4, 1, 2)
-            gate_max2(1, 0, 2)
-            quant_w(1, 3)
-            evac_b(2)
-            gate_max3(1, 0, 2)
-            w2_s(4, 2, 4)
-            evac_b(3)
-            gate_sig(1, 0, 2)
-            quant_w(1, 4)
-            gate_max1(1, 2, 4)
-            evac_z(1)
-            w2_s(5, 1, 3)
-            gate_max2(1, 2, 4)
-            gate_max3(1, 2, 4)
-            gate_sig(1, 2, 4)
-            w2_s(5, 3, 4)
-            for h in range(3):
-                gate_mul(1, h)
-            quant_w(1, 5)
-            for h in range(3, 6):
-                gate_mul(1, h)
-            quant_e(1, 0, 4)
-            quant_e(1, 4, 6)
+            quant_x(1)
+            sweep(0, 0)
+            turn_x(0, 2)
+            turn_x(1, 2)
+            w1_s(JO[1], 3, 4)
+            quant_x2(0)
+            w1_v(JO[1], 0, 3)
+            copy_x(0, 2, "s")
+            copy_x(1, 2, "s")
+            quant_x2(1)
+            quant_w(0, JO[1])
+            sweep(1, 0)
+            sweep(0, 1)
+            sweep(1, 1)
+            w1_s(JO[2], 2, 4)
+            w1_v(JO[2], 0, 2)
+            w1_v(JO[3], 0, 2)
+            quant_w(0, JO[2])
+            w1_s(JO[3], 2, 4)
+            quant_x(2)
+            quant_x2(2)
+            w1_v(JO[4], 0, 2)
+            sweep(0, 2)
+            sweep(1, 2)
+            w1_s(JO[4], 2, 4)
+            quant_w(0, JO[3])
+            sweep(0, 3)
+            sweep(1, 3)
+            w1_v(JO[5], 0, 2)
+            w1_s(JO[5], 2, 4)
+            quant_w(0, JO[4])
+            w2_v(0, 0, 2)
+            w2_s(0, 2, 4)
+            quant_w(0, JO[5])
+            for slot in range(SLOTS):
+                for pair in range(2):
+                    finish(slot, pair)
 
-            group_bank = (2, 4, 5, 6, 0, 7)
-            turn_bank = (1, 3)
+            w2_s(1, 2, 4)
+            w2_v(1, 0, 2)
+            quant_w(1, 0)
+            w2_s(3, 2, 4)
+            quant_w(1, 1)
+            w2_v(2, 0, 4)
+            evac_p(0, 0, "s")
+            evac_p(0, 1, "s")
+            w2_v(3, 0, 2)
+            quant_w(1, 2)
+            max1(0, 1)
+            quant_w(1, 3)
+            evac_p(1, 0, "s")
+            evac_p(1, 1, "s")
+            max1(1, 2)
+            w2_v(4, 0, 1)
+            evac_p(2, 0, "s")
+            evac_p(2, 1, "s")
+            max1(2, 3)
+            evac_p(3, 0, "s")
+            evac_p(3, 1, "s")
+            max1(3, 4)
+            for b in range(2):
+                for slot in range(SLOTS):
+                    single(b, slot)
+            evac_s(0, 0, "s")
+            evac_s(0, 1, "s")
+            max2(0, 0, 2)
+            w2_v(5, 0, 1)
+            max3(0, 0, 2)
+            evac_s(0, 2, "s")
+            w2_s(4, 1, 2)
+            evac_s(0, 3, "s")
+            gate_sig(0, 0, 2)
+            max2(0, 2, 4)
+            max3(0, 2, 4)
+            evac_s(1, 0, "s")
+            gate_sig(0, 2, 4)
+            max2(1, 0, 1)
+            gate_mul(0, 0)
+            quant_e(0, 0, 1)
+            evac_s(1, 1, "s")
+            gate_mul(0, 1)
+            max2(1, 1, 2)
+            quant_e(0, 1, 2)
+            w2_s(4, 2, 3)
+            evac_s(1, 2, "s")
+            gate_mul(0, 2)
+            max3(1, 0, 2)
+            quant_e(0, 2, 3)
+            w2_s(4, 3, 4)
+            evac_s(1, 3, "s")
+            gate_sig(1, 0, 2)
+            w2_s(5, 1, 4)
+            gate_mul(0, 3)
+            gate_mul(0, 4)
+            quant_e(0, 3, 4)
+            gate_mul(0, 5)
+            quant_e(0, 4, 5)
+            max2(1, 2, 4)
+            quant_e(0, 5, 6)
+            max3(1, 2, 4)
+            gate_sig(1, 2, 4)
+            quant_w(1, 4)
+            quant_w(1, 5)
+            gate_mul(1, 0)
+            gate_mul(1, 1)
+            for h in range(2, G):
+                quant_e(1, h - 2, h - 1)
+                gate_mul(1, h)
+            quant_e(1, 4, 5)
+            quant_e(1, 5, 6)
+
+            group_bank = order[0:6]
+            turn_bank = order[6:8]
             count = [0]
 
             def turns(b, q):
@@ -437,49 +474,49 @@ def tile_dihedralthreegroupblock_x1_kernel(tc, x, w1, b1, ls, w2, out, out_words
                 return t
 
             acc2 = [bank(group_bank[g]) for g in range(G)]
-            for j in range(4):
-                for g in range(G):
-                    mm2(0, acc2[g][:], g, j, j == 0, False)
+            opened = set()
+            for h in range(G):
+                for j in range(4):
+                    g = [k for k in range(G) if K[h][k] == j][0]
+                    mm2(0, acc2[g][:], g, j, g not in opened, False)
+                    opened.add(g)
             for g in range(G):
                 for j in range(4, G):
                     mm2(0, acc2[g][:], g, j, False, j == G - 1)
                 evac2(0, g, acc2[g][:])
                 cast2(0, g)
-
-            def conv2(b, g):
-                t = bank(group_bank[g])
-                for j in range(G):
-                    mm2(b, t[:], g, j, j == 0, j == G - 1)
-                evac2(b, g, t[:])
-                cast2(b, g)
-
-            conv2(1, 0)
-            conv2(1, 1)
+            acc2 = [bank(group_bank[g]) for g in range(G)]
+            for h in range(3):
+                for g in range(G):
+                    mm2(1, acc2[g][:], g, K[h][g], h == 0, False)
             t = turns(0, 0)
             s = turns(0, 1)
-            copy2(0, 0, t, "v")
+            copy2(0, 0, t, "s")
             copy2(0, 1, s, "v")
-            conv2(1, 2)
-            conv2(1, 3)
-            t = turns(0, 2)
-            s = turns(1, 0)
-            copy2(0, 2, t, "v")
-            copy2(1, 0, s, "v")
-            quant_r(0, 0, 512)
-            quant_r(0, 512, 768)
-            store_words(0, 0, 768)
-            store_scales(0, nc.sync)
-            conv2(1, 4)
-            last = bank(group_bank[5])
-            for j in range(G):
-                mm2(1, last[:], 5, j, j == 0, j == G - 1)
-            cast2(1, 5, last[:])
+            for g in range(G):
+                for h in range(3, G):
+                    mm2(1, acc2[g][:], g, K[h][g], False, h == G - 1)
+                if g < G - 1:
+                    evac2(1, g, acc2[g][:])
+                    cast2(1, g)
+                if g == 0:
+                    t = turns(0, 2)
+                    copy2(0, 2, t, "v")
+                if g == 1:
+                    quant_r(0, 0, 512)
+                    quant_r(0, 512, 768)
+                    store_words(0, 0, 768)
+                    store_scales(0, nc.sync)
+                if g == 3:
+                    t = turns(1, 0)
+                    copy2(1, 0, t, "s")
+            cast2(1, 5, acc2[5][:])
             t = turns(1, 1)
             s = turns(1, 2)
             copy2(1, 1, t, "s")
-            evac2(1, 5, last[:])
-            copy2(1, 2, s, "v", 0, 64)
-            copy2(1, 2, s, "v", 64, P)
+            evac2(1, 5, acc2[5][:], "v")
+            copy2(1, 2, s, "s", 0, 64)
+            copy2(1, 2, s, "s", 64, P)
             quant_r(1, 0, 256)
             quant_r(1, 256, 384)
             store_words(1, 0, 384)

@@ -288,8 +288,6 @@ def tile_dihedralthreegroupblock_x1_kernel(tc, x, w1, b1, ls, w2, out, out_words
             nc.vector.memset(warm[:], 0.0)
             nc.scalar.activation(out=warm[:], in_=warm[:], func=ACT.Sigmoid)
             nc.vector.memset(zeros[:], 0.0)
-            nc.scalar.dma_start(out=b1_raw[:], in_=b1.rearrange("(p t) -> p t", t=4))
-            nc.scalar.dma_start(out=ls_raw[:], in_=ls.rearrange("(p t) -> p t", t=4))
             cold = bank(7)
 
             def warm_up(n):
@@ -297,8 +295,6 @@ def tile_dihedralthreegroupblock_x1_kernel(tc, x, w1, b1, ls, w2, out, out_words
                     nc.tensor.matmul(cold[:], lhsT=zeros[:, 0:P], rhs=zeros[:], start=True, stop=True)
 
             warm_up(4)
-            nc.scalar.copy(out=b1_col[:], in_=b1_raw[:])
-            nc.scalar.copy(out=ls_col[:], in_=ls_raw[:])
             load_x(0, 0)
             load_x(1, 0)
             load_w(0, JO[0])
@@ -308,6 +304,8 @@ def tile_dihedralthreegroupblock_x1_kernel(tc, x, w1, b1, ls, w2, out, out_words
             load_x(1, 2)
             for i in range(1, G):
                 load_w(0, JO[i])
+            nc.sync.dma_start(out=b1_raw[:], in_=b1.rearrange("(p t) -> p t", t=4))
+            nc.sync.dma_start(out=ls_raw[:], in_=ls.rearrange("(p t) -> p t", t=4))
             for j in range(G):
                 load_w(1, j)
 
@@ -339,13 +337,13 @@ def tile_dihedralthreegroupblock_x1_kernel(tc, x, w1, b1, ls, w2, out, out_words
             turn_x(0, 0)
             turn_x(1, 0)
             copy_x(0, 0, "s")
-            copy_x(1, 0, "s")
-            w1_v(JO[0], 0, 3)
-            w1_s(JO[0], 3, 4)
+            copy_x(1, 0, "v")
+            w1_v(JO[0], 0, 2)
+            w1_s(JO[0], 2, 4)
             warm_up(2)
             turn_x(0, 1)
             turn_x(1, 1)
-            warm_up(2)
+            warm_up(1)
             quant_x(0)
             quant_w(0, JO[0], 0, 2)
             quant_w(0, JO[0], 2, 4)
@@ -395,6 +393,8 @@ def tile_dihedralthreegroupblock_x1_kernel(tc, x, w1, b1, ls, w2, out, out_words
             w2_s(3, 2, 4)
             quant_w(1, 1)
             w2_v(2, 0, 4)
+            nc.scalar.copy(out=b1_col[:], in_=b1_raw[:])
+            nc.scalar.copy(out=ls_col[:], in_=ls_raw[:])
             evac_p(0, 0, "s")
             evac_p(0, 1, "s")
             w2_v(3, 0, 2)
@@ -423,12 +423,15 @@ def tile_dihedralthreegroupblock_x1_kernel(tc, x, w1, b1, ls, w2, out, out_words
             w2_s(4, 1, 2)
             evac_s(0, 3, "s")
             gate_sig(0, 0, 2)
-            max2(0, 2, 4)
-            max3(0, 2, 4)
+            max2(0, 2, 3)
+            max2(0, 3, 4)
+            max3(0, 2, 3)
+            gate_sig(0, 2, 3)
+            max3(0, 3, 4)
+            gate_sig(0, 3, 4)
             evac_s(1, 0, "s")
-            gate_sig(0, 2, 4)
-            max2(1, 0, 1)
             gate_mul(0, 0)
+            max2(1, 0, 1)
             quant_e(0, 0, 1)
             evac_s(1, 1, "s")
             gate_mul(0, 1)
@@ -444,13 +447,14 @@ def tile_dihedralthreegroupblock_x1_kernel(tc, x, w1, b1, ls, w2, out, out_words
             gate_sig(1, 0, 2)
             w2_s(5, 1, 4)
             gate_mul(0, 3)
-            gate_mul(0, 4)
+            max2(1, 2, 3)
             quant_e(0, 3, 4)
-            gate_mul(0, 5)
+            gate_mul(0, 4)
+            max2(1, 3, 4)
             quant_e(0, 4, 5)
-            max2(1, 2, 4)
-            quant_e(0, 5, 6)
+            gate_mul(0, 5)
             max3(1, 2, 4)
+            quant_e(0, 5, 6)
             gate_sig(1, 2, 4)
             quant_w(1, 4)
             quant_w(1, 5)
@@ -489,10 +493,11 @@ def tile_dihedralthreegroupblock_x1_kernel(tc, x, w1, b1, ls, w2, out, out_words
             for h in range(3):
                 for g in range(G):
                     mm2(1, acc2[g][:], g, K[h][g], h == 0, False)
-            t = turns(0, 0)
-            s = turns(0, 1)
-            copy2(0, 0, t, "s")
-            copy2(0, 1, s, "v")
+                if h == 1:
+                    t = turns(0, 0)
+                    s = turns(0, 1)
+                    copy2(0, 0, t, "s")
+                    copy2(0, 1, s, "v")
             for g in range(G):
                 for h in range(3, G):
                     mm2(1, acc2[g][:], g, K[h][g], False, h == G - 1)

@@ -23,8 +23,8 @@ K = (
     (4, 3, 5, 1, 0, 2),
     (5, 4, 3, 2, 1, 0),
 )
-PAIRS = ((0, 3), (1, 5), (2, 4))
-JO = (0, 5, 1, 2, 3, 4)
+PAIRS = ((2, 3), (0, 5), (1, 4))
+JO = (0, 3, 1, 2, 4, 5)
 P = 128
 SLOTS = 4
 
@@ -196,11 +196,25 @@ def tile_dihedralthreegroupblock_x1_kernel(tc, x, w1, b1, ls, w2, out, out_words
         def max2(b, lo, hi):
             nc.vector.tensor_tensor(out=t2[b][:, lo:hi], in0=t1[:, lo:hi, :, tok(b)], in1=y[:, lo:hi, 2, :, tok(b)], op=ALU.max)
 
+        last = {}
+
+        def max2_psum(b, slot):
+            nc.vector.scalar_tensor_tensor(
+                out=t2[b][:, slot],
+                in0=last[b, slot][:, 0 : 2 * P].rearrange("p (m n) -> p m n", m=2),
+                scalar=b1_col[:, slot : slot + 1],
+                in1=t1[:, slot, :, tok(b)],
+                op0=ALU.add,
+                op1=ALU.max,
+            )
+
         def max3(b, lo, hi):
             nc.vector.tensor_tensor(out=top[b][:, lo:hi], in0=t2[b][:, lo:hi, 0], in1=t2[b][:, lo:hi, 1], op=ALU.max)
 
         def gate_sig(b, lo, hi):
             nc.scalar.activation(out=sig[b][:, lo:hi], in_=top[b][:, lo:hi], func=ACT.Sigmoid)
+
+        def gate_fac(b, lo, hi):
             for s in range(lo, hi):
                 nc.scalar.activation(out=fac[b][:, s], in_=sig[b][:, s], func=ACT.Copy, scale=ls_col[:, s : s + 1])
 
@@ -245,7 +259,7 @@ def tile_dihedralthreegroupblock_x1_kernel(tc, x, w1, b1, ls, w2, out, out_words
 
         def cast2(b, g, src=None):
             src = res["o", b, g][:] if src is None else src
-            o = sb([P, C], BF16, "obf", bufs=8)
+            o = sb([P, C], BF16, "obf", bufs=6)
             nc.vector.tensor_copy(
                 out=o[:].rearrange("p (u w e) -> p u w e", u=2, e=2),
                 in_=src.rearrange("p (w u e) -> p u w e", u=2, e=2),
@@ -325,7 +339,6 @@ def tile_dihedralthreegroupblock_x1_kernel(tc, x, w1, b1, ls, w2, out, out_words
             def evac_p(slot, pair, eng):
                 evac1(y[:, slot, pair].rearrange("p m n -> p (m n)"), acc[slot, pair][:], slot, eng)
 
-            last = {}
             def single(b, slot):
                 last[b, slot] = bank(order[4 * b + slot])
                 for m in range(2):
@@ -365,11 +378,11 @@ def tile_dihedralthreegroupblock_x1_kernel(tc, x, w1, b1, ls, w2, out, out_words
             sweep(1, 1)
             w1_s(JO[2], 2, 4)
             w1_v(JO[2], 0, 2)
-            w1_v(JO[3], 0, 2)
-            quant_w(0, JO[2])
-            w1_s(JO[3], 2, 4)
             quant_x(2)
             quant_x2(2)
+            quant_w(0, JO[2])
+            w1_v(JO[3], 0, 2)
+            w1_s(JO[3], 2, 4)
             w1_v(JO[4], 0, 2)
             sweep(0, 2)
             sweep(1, 2)
@@ -398,13 +411,11 @@ def tile_dihedralthreegroupblock_x1_kernel(tc, x, w1, b1, ls, w2, out, out_words
             evac_p(0, 0, "s")
             evac_p(0, 1, "s")
             w2_v(3, 0, 2)
-            quant_w(1, 2)
             max1(0, 1)
-            quant_w(1, 3)
+            quant_w(1, 2)
             evac_p(1, 0, "s")
             evac_p(1, 1, "s")
             max1(1, 2)
-            w2_v(4, 0, 1)
             evac_p(2, 0, "s")
             evac_p(2, 1, "s")
             max1(2, 3)
@@ -416,20 +427,22 @@ def tile_dihedralthreegroupblock_x1_kernel(tc, x, w1, b1, ls, w2, out, out_words
                     single(b, slot)
             evac_s(0, 0, "s")
             evac_s(0, 1, "s")
+            w2_s(4, 0, 1)
             max2(0, 0, 2)
-            w2_v(5, 0, 1)
-            max3(0, 0, 2)
-            evac_s(0, 2, "s")
+            max2_psum(0, 2)
             w2_s(4, 1, 2)
-            evac_s(0, 3, "s")
-            gate_sig(0, 0, 2)
-            max2(0, 2, 3)
-            max2(0, 3, 4)
+            evac_s(0, 2, "s")
+            max3(0, 0, 2)
             max3(0, 2, 3)
-            gate_sig(0, 2, 3)
+            gate_sig(0, 0, 2)
+            gate_fac(0, 0, 2)
+            max2_psum(0, 3)
             max3(0, 3, 4)
-            gate_sig(0, 3, 4)
+            gate_sig(0, 2, 4)
+            evac_s(0, 3, "s")
+            gate_fac(0, 2, 4)
             evac_s(1, 0, "s")
+            quant_w(1, 3)
             gate_mul(0, 0)
             max2(1, 0, 1)
             quant_e(0, 0, 1)
@@ -442,21 +455,23 @@ def tile_dihedralthreegroupblock_x1_kernel(tc, x, w1, b1, ls, w2, out, out_words
             gate_mul(0, 2)
             max3(1, 0, 2)
             quant_e(0, 2, 3)
-            w2_s(4, 3, 4)
             evac_s(1, 3, "s")
+            w2_s(4, 3, 4)
             gate_sig(1, 0, 2)
-            w2_s(5, 1, 4)
+            gate_fac(1, 0, 2)
+            w2_s(5, 0, 4)
             gate_mul(0, 3)
-            max2(1, 2, 3)
+            quant_w(1, 4)
             quant_e(0, 3, 4)
             gate_mul(0, 4)
-            max2(1, 3, 4)
+            max2(1, 2, 3)
             quant_e(0, 4, 5)
             gate_mul(0, 5)
-            max3(1, 2, 4)
+            max2(1, 3, 4)
             quant_e(0, 5, 6)
+            max3(1, 2, 4)
             gate_sig(1, 2, 4)
-            quant_w(1, 4)
+            gate_fac(1, 2, 4)
             quant_w(1, 5)
             gate_mul(1, 0)
             gate_mul(1, 1)
@@ -466,59 +481,55 @@ def tile_dihedralthreegroupblock_x1_kernel(tc, x, w1, b1, ls, w2, out, out_words
             quant_e(1, 4, 5)
             quant_e(1, 5, 6)
 
-            group_bank = order[0:6]
-            turn_bank = order[6:8]
-            count = [0]
-
-            def turns(b, q):
-                t = bank(turn_bank[count[0] % 2])
-                count[0] += 1
+            def turns(b, q, i):
+                t = bank(order[i])
                 turn2(b, 2 * q, t)
                 turn2(b, 2 * q + 1, t)
                 return t
 
-            acc2 = [bank(group_bank[g]) for g in range(G)]
+            acc2 = [bank(order[g]) for g in range(G)]
+            early = [(h, j) for h in range(G) for j in range(4 if h < 3 else 5)]
             opened = set()
-            for h in range(G):
-                for j in range(4):
-                    g = [k for k in range(G) if K[h][k] == j][0]
-                    mm2(0, acc2[g][:], g, j, g not in opened, False)
-                    opened.add(g)
+            for h, j in early:
+                g = [k for k in range(G) if K[h][k] == j][0]
+                mm2(0, acc2[g][:], g, j, g not in opened, False)
+                opened.add(g)
             for g in range(G):
                 for j in range(4, G):
-                    mm2(0, acc2[g][:], g, j, False, j == G - 1)
+                    if (element(j, g), j) not in early:
+                        mm2(0, acc2[g][:], g, j, False, j == G - 1)
                 evac2(0, g, acc2[g][:])
                 cast2(0, g)
-            acc2 = [bank(group_bank[g]) for g in range(G)]
+            acc2 = [bank(order[g]) for g in range(G - 1)]
             for h in range(3):
-                for g in range(G):
+                for g in range(G - 1):
                     mm2(1, acc2[g][:], g, K[h][g], h == 0, False)
-                if h == 1:
-                    t = turns(0, 0)
-                    s = turns(0, 1)
-                    copy2(0, 0, t, "s")
-                    copy2(0, 1, s, "v")
-            for g in range(G):
+            ts = [turns(0, 0, 6), turns(0, 1, 7), turns(0, 2, 5)]
+            copy2(0, 0, ts[0], "s")
+            copy2(0, 1, ts[1], "v")
+            copy2(0, 2, ts[2], "v")
+            acc2.append(bank(order[6]))
+            for g in range(G - 1):
                 for h in range(3, G):
                     mm2(1, acc2[g][:], g, K[h][g], False, h == G - 1)
-                if g < G - 1:
-                    evac2(1, g, acc2[g][:])
-                    cast2(1, g)
+                evac2(1, g, acc2[g][:])
+                cast2(1, g)
                 if g == 0:
-                    t = turns(0, 2)
-                    copy2(0, 2, t, "v")
-                if g == 1:
                     quant_r(0, 0, 512)
+                if g == 1:
                     quant_r(0, 512, 768)
                     store_words(0, 0, 768)
                     store_scales(0, nc.sync)
-                if g == 3:
-                    t = turns(1, 0)
-                    copy2(1, 0, t, "s")
+            for h in range(3):
+                mm2(1, acc2[5][:], 5, K[h][5], h == 0, False)
+            t = turns(1, 0, 7)
+            s = turns(1, 1, 5)
+            copy2(1, 0, t, "s")
+            copy2(1, 1, s, "v")
+            for h in range(3, G):
+                mm2(1, acc2[5][:], 5, K[h][5], False, h == G - 1)
             cast2(1, 5, acc2[5][:])
-            t = turns(1, 1)
-            s = turns(1, 2)
-            copy2(1, 1, t, "s")
+            s = turns(1, 2, 0)
             evac2(1, 5, acc2[5][:], "v")
             copy2(1, 2, s, "s", 0, 64)
             copy2(1, 2, s, "s", 64, P)

from contextlib import ExitStack

import concourse.mybir as mybir
from concourse.masks import make_identity

F32 = mybir.dt.float32
BF16 = mybir.dt.bfloat16
U32 = mybir.dt.uint32
I32 = mybir.dt.int32
U8 = mybir.dt.uint8
FP8X4 = mybir.dt.float8_e4m3fn_x4
ACT = mybir.ActivationFunctionType
ALU = mybir.AluOpType

N, G, C = 256, 6, 512
FLOPS = 2 * (2 * N * G * G * C * C)

K = (
    (0, 1, 2, 3, 4, 5),
    (2, 0, 1, 5, 3, 4),
    (1, 2, 0, 4, 5, 3),
    (3, 5, 4, 0, 2, 1),
    (4, 3, 5, 1, 0, 2),
    (5, 4, 3, 2, 1, 0),
)
PAIRS = ((2, 3), (0, 5), (1, 4))
JO = (0, 3, 1, 2, 4, 5)
P = 128
SLOTS = 4


def source(pair, j):
    a, b = PAIRS[pair]
    h = [k for k in range(G) if K[k][a] == j][0]
    h2 = [k for k in range(G) if K[k][b] == j][0]
    for q, (c, e) in enumerate(PAIRS):
        if (h, h2) == (c, e):
            return q, 0
        if (h, h2) == (e, c):
            return q, 1
    raise ValueError("not a pair")


def element(j, g):
    return [h for h in range(G) if K[h][g] == j][0]


def place(h):
    for q, pr in enumerate(PAIRS):
        if h in pr:
            return q, pr.index(h)
    raise ValueError("no such element")


def tile_dihedralthreegroupblock_x1_kernel(tc, x, w1, b1, ls, w2, out, out_words, out_scales):
    nc = tc.nc
    with ExitStack() as ctx:
        const = ctx.enter_context(tc.tile_pool(name="const", bufs=1))
        stage = ctx.enter_context(tc.tile_pool(name="stage", bufs=1))
        psum = ctx.enter_context(tc.psum_pool(name="psum", bufs=1))

        def sb(shape, dtype, name, bufs=1):
            return stage.tile(shape, dtype, name=name, bufs=bufs, align_bytes=64)

        def bank(i):
            return psum.tile([P, 512], F32, name="bank%d" % i)

        ident = const.tile([P, P], F32, name="ident", align_bytes=64)
        make_identity(nc, ident[:])
        b1_raw = const.tile([P, SLOTS], BF16, name="b1_raw")
        ls_raw = const.tile([P, SLOTS], BF16, name="ls_raw")
        b1_col = const.tile([P, SLOTS], F32, name="b1_col")
        ls_col = const.tile([P, SLOTS], F32, name="ls_col")
        warm = const.tile([P, 2], F32, name="warm")
        zeros = const.tile([P, C], BF16, name="zeros", align_bytes=64)

        x_raw = [sb([P, G, C], BF16, "x_raw%d" % b) for b in range(2)]
        w_raw = [[sb([P, 4, C], BF16, "w%d_raw%d" % (s, j)) for j in range(G)] for s in range(2)]
        x_il = [sb([P, 2, N, 4], BF16, "x_il%d" % q) for q in range(3)]
        x_cod = [sb([P, 3 * N], U32, "x_cod%d" % q) for q in range(3)]
        x_sca = [sb([P, 3 * N], U8, "x_sca%d" % q) for q in range(3)]
        w_cod = [[sb([P, C], U32, "w%d_cod%d" % (s, j)) for j in range(G)] for s in range(2)]
        w_sca = [[sb([P, C], U8, "w%d_sca%d" % (s, j)) for j in range(G)] for s in range(2)]
        y = sb([P, SLOTS, 3, 2, N], F32, "y")
        t1 = sb([P, SLOTS, 2, N], F32, "t1")
        t2 = [sb([P, SLOTS, 2, P], F32, "t2"), None]
        t2[1] = t2[0]
        top = [sb([P, SLOTS, P], F32, "top%d" % b) for b in range(2)]
        sig = [sb([P, SLOTS, P], F32, "sig%d" % b) for b in range(2)]
        fac = [sb([P, SLOTS, P], F32, "fac%d" % b) for b in range(2)]
        e_il = [sb([P, G, P, 4], BF16, "e_il%d" % b) for b in range(2)]
        e_cod = [sb([P, G, P], U32, "e_cod%d" % b) for b in range(2)]
        e_sca = [sb([P, G, P], U8, "e_sca%d" % b) for b in range(2)]
        r_il = [sb([P, P, G, 4], BF16, "r_il%d" % b) for b in range(2)]
        r_cod = [sb([P, P * G], U32, "r_cod%d" % b) for b in range(2)]
        r_sca = [sb([P, P * G], U8, "r_sca%d" % b) for b in range(2)]
        w_il = {}

        def tok(b):
            return slice(b * P, (b + 1) * P)

        def load_x(b, q):
            lo, hi = PAIRS[q]
            nc.sync.dma_start(out=x_raw[b][:, lo : hi + 1 : hi - lo, :], in_=x[tok(b), lo : hi + 1 : hi - lo, :])

        def load_w(s, j):
            w = (w1, w2)[s]
            nc.sync.dma_start(out=w_raw[s][j][:], in_=w[j].rearrange("(p t) d -> p t d", t=4))

        x_bank = {}

        def turn_x(b, q):
            t = bank(2 * q + b)
            x_bank[b, q] = t
            words = x_raw[b][:].rearrange("p g c -> p (g c)").bitcast(F32)
            for m, h in enumerate(PAIRS[q]):
                for u in range(2):
                    nc.tensor.transpose(t[:, (2 * m + u) * P : (2 * m + u + 1) * P], words[:, 256 * h + u : 256 * (h + 1) : 2], ident[:])

        def copy_x(b, q, eng):
            src = x_bank[b, q][:].rearrange("p (m u n) -> p m n u", m=2, u=2)
            dst = x_il[q][:].rearrange("p m n t -> p (m n t)").bitcast(F32).rearrange("p (m n u) -> p m n u", m=2, u=2)[:, :, tok(b)]
            if eng == "v":
                nc.vector.tensor_copy(out=dst, in_=src)
            else:
                nc.scalar.copy(out=dst, in_=src)

        def quant(cod, sca, src):
            nc.vector.quantize_mx(out=cod.bitcast(FP8X4), scales=sca, in_=src)

        def quant_x(q):
            flat = x_il[q][:].rearrange("p m n t -> p (m n t)")
            quant(x_cod[q][:, 0 : 2 * N], x_sca[q][:, 0 : 2 * N], flat)

        def quant_x2(q):
            flat = x_il[q][:].rearrange("p m n t -> p (m n t)")
            quant(x_cod[q][:, 2 * N : 3 * N], x_sca[q][:, 2 * N : 3 * N], flat[:, 0 : 4 * N])

        def il_w(s, j, lo, hi, eng):
            if (s, j) not in w_il:
                w_il[s, j] = sb([P, 4 * C], BF16, "w_il", bufs=3)
            pat = ("p (t m k) -> p m k t", "p (m t k) -> p m k t")[s]
            d = w_il[s, j][:].rearrange(pat, t=4, k=4)[:, lo * 32 : hi * 32]
            v = w_raw[s][j][:].rearrange("p k (m t) -> p m k t", t=4)[:, lo * 32 : hi * 32]
            if eng == "v":
                nc.vector.tensor_copy(out=d, in_=v)
            else:
                nc.scalar.copy(out=d, in_=v)

        def w1_v(j, lo, hi):
            il_w(0, j, lo, hi, "v")

        def w1_s(j, lo, hi):
            il_w(0, j, lo, hi, "s")

        def w2_v(j, lo, hi):
            il_w(1, j, lo, hi, "v")

        def w2_s(j, lo, hi):
            il_w(1, j, lo, hi, "s")

        def quant_w(s, j, lo=0, hi=4):
            quant(w_cod[s][j][:, lo * P : hi * P], w_sca[s][j][:, lo * P : hi * P], w_il[s, j][:, lo * C : hi * C])

        def mm1(dst, slot, j, q, cols, start, stop):
            sl = slice(slot * P, (slot + 1) * P)
            nc.tensor.matmul_mx(
                out=dst,
                lhsT=w_cod[0][j][:, sl].bitcast(FP8X4),
                lhsT_scale=w_sca[0][j][:, sl],
                rhs=x_cod[q][:, cols].bitcast(FP8X4),
                rhs_scale=x_sca[q][:, cols],
                start=start,
                stop=stop,
            )

        def pair_pass(dst, slot, pair, j, start, stop):
            q, turned = source(pair, j)
            mm1(dst, slot, j, q, slice(turned * N, turned * N + 2 * N), start, stop)

        def single_group(dst, slot, g, b):
            for j in range(G):
                q, m = place(element(j, g))
                mm1(dst, slot, j, q, slice(m * N + b * P, m * N + (b + 1) * P), j == 0, j == G - 1)

        def evac1(dst, src, slot, eng):
            bias = b1_col[:, slot : slot + 1]
            if eng == "v":
                nc.vector.tensor_scalar(out=dst, in0=src, scalar1=bias, scalar2=None, op0=ALU.add)
            else:
                nc.scalar.activation(out=dst, in_=src, func=ACT.Identity, bias=bias)

        def max1(lo, hi):
            nc.vector.tensor_tensor(out=t1[:, lo:hi], in0=y[:, lo:hi, 0], in1=y[:, lo:hi, 1], op=ALU.max)

        def max2(b, lo, hi):
            nc.vector.tensor_tensor(out=t2[b][:, lo:hi], in0=t1[:, lo:hi, :, tok(b)], in1=y[:, lo:hi, 2, :, tok(b)], op=ALU.max)

        last = {}

        def max2_psum(b, slot):
            nc.vector.scalar_tensor_tensor(
                out=t2[b][:, slot],
                in0=last[b, slot][:, 0 : 2 * P].rearrange("p (m n) -> p m n", m=2),
                scalar=b1_col[:, slot : slot + 1],
                in1=t1[:, slot, :, tok(b)],
                op0=ALU.add,
                op1=ALU.max,
            )

        def max3(b, lo, hi):
            nc.vector.tensor_tensor(out=top[b][:, lo:hi], in0=t2[b][:, lo:hi, 0], in1=t2[b][:, lo:hi, 1], op=ALU.max)

        def gate_sig(b, lo, hi):
            nc.scalar.activation(out=sig[b][:, lo:hi], in_=top[b][:, lo:hi], func=ACT.Sigmoid)

        def gate_fac(b, lo, hi):
            for s in range(lo, hi):
                nc.scalar.activation(out=fac[b][:, s], in_=sig[b][:, s], func=ACT.Copy, scale=ls_col[:, s : s + 1])

        def gate_mul(b, h):
            q, m = place(h)
            nc.vector.tensor_tensor(
                out=e_il[b][:, h].rearrange("p (c i) s -> p c s i", i=4),
                in0=y[:, :, q, m, tok(b)].rearrange("p s (c i) -> p c s i", i=4),
                in1=fac[b][:].rearrange("p s (c i) -> p c s i", i=4),
                op=ALU.mult,
            )

        def quant_e(b, lo, hi):
            quant(
                e_cod[b][:, lo:hi].rearrange("p h n -> p (h n)"),
                e_sca[b][:, lo:hi].rearrange("p h n -> p (h n)"),
                e_il[b][:, lo:hi].rearrange("p h n t -> p (h n t)"),
            )

        def mm2(b, dst, g, j, start, stop):
            h = element(j, g)
            nc.tensor.matmul_mx(
                out=dst,
                lhsT=e_cod[b][:, h].bitcast(FP8X4),
                lhsT_scale=e_sca[b][:, h],
                rhs=w_cod[1][j][:].bitcast(FP8X4),
                rhs_scale=w_sca[1][j][:],
                start=start,
                stop=stop,
            )

        res = {}

        def evac2(b, g, src, eng="s"):
            o = sb([P, C], F32, "o32", bufs=6)
            if eng == "v":
                nc.vector.tensor_copy(out=o[:], in_=src)
            else:
                nc.scalar.copy(out=o[:], in_=src)
            nc.sync.dma_start(out=out[b * P : (b + 1) * P, g, :], in_=o[:])
            res["o", b, g] = o

        def cast2(b, g, src=None):
            src = res["o", b, g][:] if src is None else src
            o = sb([P, C], BF16, "obf", bufs=6)
            nc.vector.tensor_copy(
                out=o[:].rearrange("p (u w e) -> p u w e", u=2, e=2),
                in_=src.rearrange("p (w u e) -> p u w e", u=2, e=2),
            )
            res["b", b, g] = o

        def turn2(b, g, dst):
            words = res["b", b, g][:].bitcast(F32)
            for u in range(2):
                i = 2 * (g % 2) + u
                nc.tensor.transpose(dst[:, i * P : (i + 1) * P], words[:, u * P : (u + 1) * P], ident[:])

        def copy2(b, q, src, eng, lo=0, hi=P):
            d = r_il[b][:].rearrange("p n g t -> p (n g t)").bitcast(F32).rearrange("p (n q i) -> p n q i", q=3, i=4)[:, lo:hi, q]
            v = src[:].rearrange("p (i n) -> p n i", i=4)[:, lo:hi]
            if eng == "v":
                nc.vector.tensor_copy(out=d, in_=v)
            else:
                nc.scalar.copy(out=d, in_=v)

        def quant_r(b, lo, hi):
            flat = r_il[b][:].rearrange("p n g t -> p (n g t)")
            quant(r_cod[b][:, lo:hi], r_sca[b][:, lo:hi], flat[:, 4 * lo : 4 * hi])

        def store_words(b, lo, hi):
            nc.sync.dma_start(
                out=out_words[0, :, b * P * G + lo : b * P * G + hi, :].rearrange("p m t -> p (m t)").bitcast(I32),
                in_=r_cod[b][:, lo:hi].bitcast(I32),
            )

        def store_scales(b, eng):
            cols = slice(b * P * G, (b + 1) * P * G)
            for k in range(4):
                eng.dma_start(
                    out=out_scales[0, 4 * k : 4 * k + 4, cols].bitcast(I32),
                    in_=r_sca[b][32 * k : 32 * k + 4, :].bitcast(I32),
                )

        with tc.manual_schedule():
            nc.vector.memset(warm[:], 0.0)
            nc.scalar.activation(out=warm[:], in_=warm[:], func=ACT.Sigmoid)
            nc.vector.memset(zeros[:], 0.0)
            cold = bank(7)

            def warm_up(n):
                for i in range(n):
                    nc.tensor.matmul(cold[:], lhsT=zeros[:, 0:P], rhs=zeros[:], start=True, stop=True)

            warm_up(4)
            load_x(0, 0)
            load_x(1, 0)
            load_w(0, JO[0])
            load_x(0, 1)
            load_x(1, 1)
            load_x(0, 2)
            load_x(1, 2)
            for i in range(1, G):
                load_w(0, JO[i])
            nc.sync.dma_start(out=b1_raw[:], in_=b1.rearrange("(p t) -> p t", t=4))
            nc.sync.dma_start(out=ls_raw[:], in_=ls.rearrange("(p t) -> p t", t=4))
            for j in range(G):
                load_w(1, j)

            acc = {}
            order = (6, 7, 0, 1, 2, 3, 4, 5)

            def sweep(pair, i):
                for slot in range(SLOTS):
                    if i == 0:
                        acc[slot, pair] = bank(order[4 * pair + slot])
                    pair_pass(acc[slot, pair][:], slot, pair, JO[i], i == 0, False)

            def finish(slot, pair):
                for i in (4, 5):
                    pair_pass(acc[slot, pair][:], slot, pair, JO[i], False, i == 5)

            def evac_p(slot, pair, eng):
                evac1(y[:, slot, pair].rearrange("p m n -> p (m n)"), acc[slot, pair][:], slot, eng)

            def single(b, slot):
                last[b, slot] = bank(order[4 * b + slot])
                for m in range(2):
                    single_group(last[b, slot][:, m * P : (m + 1) * P], slot, PAIRS[2][m], b)

            def evac_s(b, slot, eng):
                evac1(y[:, slot, 2, :, tok(b)], last[b, slot][:, 0 : 2 * P].rearrange("p (m n) -> p m n", m=2), slot, eng)

            turn_x(0, 0)
            turn_x(1, 0)
            copy_x(0, 0, "s")
            copy_x(1, 0, "v")
            w1_v(JO[0], 0, 2)
            w1_s(JO[0], 2, 4)
            warm_up(2)
            turn_x(0, 1)
            turn_x(1, 1)
            warm_up(1)
            quant_x(0)
            quant_w(0, JO[0], 0, 2)
            quant_w(0, JO[0], 2, 4)
            copy_x(0, 1, "s")
            copy_x(1, 1, "s")
            quant_x(1)
            sweep(0, 0)
            turn_x(0, 2)
            turn_x(1, 2)
            w1_s(JO[1], 3, 4)
            quant_x2(0)
            w1_v(JO[1], 0, 3)
            copy_x(0, 2, "s")
            copy_x(1, 2, "s")
            quant_x2(1)
            quant_w(0, JO[1])
            sweep(1, 0)
            sweep(0, 1)
            sweep(1, 1)
            w1_s(JO[2], 2, 4)
            w1_v(JO[2], 0, 2)
            quant_x(2)
            quant_x2(2)
            quant_w(0, JO[2])
            w1_v(JO[3], 0, 2)
            w1_s(JO[3], 2, 4)
            w1_v(JO[4], 0, 2)
            sweep(0, 2)
            sweep(1, 2)
            w1_s(JO[4], 2, 4)
            quant_w(0, JO[3])
            sweep(0, 3)
            sweep(1, 3)
            w1_v(JO[5], 0, 2)
            w1_s(JO[5], 2, 4)
            quant_w(0, JO[4])
            w2_v(0, 0, 2)
            w2_s(0, 2, 4)
            quant_w(0, JO[5])
            for slot in range(SLOTS):
                for pair in range(2):
                    finish(slot, pair)

            w2_s(1, 2, 4)
            w2_v(1, 0, 2)
            quant_w(1, 0)
            w2_s(3, 2, 4)
            quant_w(1, 1)
            w2_v(2, 0, 4)
            nc.scalar.copy(out=b1_col[:], in_=b1_raw[:])
            nc.scalar.copy(out=ls_col[:], in_=ls_raw[:])
            evac_p(0, 0, "s")
            evac_p(0, 1, "s")
            w2_v(3, 0, 2)
            max1(0, 1)
            quant_w(1, 2)
            evac_p(1, 0, "s")
            evac_p(1, 1, "s")
            max1(1, 2)
            evac_p(2, 0, "s")
            evac_p(2, 1, "s")
            max1(2, 3)
            evac_p(3, 0, "s")
            evac_p(3, 1, "s")
            max1(3, 4)
            for b in range(2):
                for slot in range(SLOTS):
                    single(b, slot)
            evac_s(0, 0, "s")
            evac_s(0, 1, "s")
            w2_s(4, 0, 1)
            max2(0, 0, 2)
            max2_psum(0, 2)
            w2_s(4, 1, 2)
            evac_s(0, 2, "s")
            max3(0, 0, 2)
            max3(0, 2, 3)
            gate_sig(0, 0, 2)
            gate_fac(0, 0, 2)
            max2_psum(0, 3)
            max3(0, 3, 4)
            gate_sig(0, 2, 4)
            evac_s(0, 3, "s")
            gate_fac(0, 2, 4)
            evac_s(1, 0, "s")
            quant_w(1, 3)
            gate_mul(0, 0)
            max2(1, 0, 1)
            quant_e(0, 0, 1)
            evac_s(1, 1, "s")
            gate_mul(0, 1)
            max2(1, 1, 2)
            quant_e(0, 1, 2)
            w2_s(4, 2, 3)
            evac_s(1, 2, "s")
            gate_mul(0, 2)
            max3(1, 0, 2)
            quant_e(0, 2, 3)
            evac_s(1, 3, "s")
            w2_s(4, 3, 4)
            gate_sig(1, 0, 2)
            gate_fac(1, 0, 2)
            w2_s(5, 0, 4)
            gate_mul(0, 3)
            quant_w(1, 4)
            quant_e(0, 3, 4)
            gate_mul(0, 4)
            max2(1, 2, 3)
            quant_e(0, 4, 5)
            gate_mul(0, 5)
            max2(1, 3, 4)
            quant_e(0, 5, 6)
            max3(1, 2, 4)
            gate_sig(1, 2, 4)
            gate_fac(1, 2, 4)
            quant_w(1, 5)
            gate_mul(1, 0)
            gate_mul(1, 1)
            for h in range(2, G):
                quant_e(1, h - 2, h - 1)
                gate_mul(1, h)
            quant_e(1, 4, 5)
            quant_e(1, 5, 6)

            def turns(b, q, i):
                t = bank(order[i])
                turn2(b, 2 * q, t)
                turn2(b, 2 * q + 1, t)
                return t

            acc2 = [bank(order[g]) for g in range(G)]
            early = [(h, j) for h in range(G) for j in range(4 if h < 3 else 5)]
            opened = set()
            for h, j in early:
                g = [k for k in range(G) if K[h][k] == j][0]
                mm2(0, acc2[g][:], g, j, g not in opened, False)
                opened.add(g)
            for g in range(G):
                for j in range(4, G):
                    if (element(j, g), j) not in early:
                        mm2(0, acc2[g][:], g, j, False, j == G - 1)
                evac2(0, g, acc2[g][:])
                cast2(0, g)
            acc2 = [bank(order[g]) for g in range(G - 1)]
            for h in range(3):
                for g in range(G - 1):
                    mm2(1, acc2[g][:], g, K[h][g], h == 0, False)
            ts = [turns(0, 0, 6), turns(0, 1, 7), turns(0, 2, 5)]
            copy2(0, 0, ts[0], "s")
            copy2(0, 1, ts[1], "v")
            copy2(0, 2, ts[2], "v")
            acc2.append(bank(order[6]))
            for g in range(G - 1):
                for h in range(3, G):
                    mm2(1, acc2[g][:], g, K[h][g], False, h == G - 1)
                evac2(1, g, acc2[g][:])
                cast2(1, g)
                if g == 0:
                    quant_r(0, 0, 512)
                if g == 1:
                    quant_r(0, 512, 768)
                    store_words(0, 0, 768)
                    store_scales(0, nc.sync)
            for h in range(3):
                mm2(1, acc2[5][:], 5, K[h][5], h == 0, False)
            t = turns(1, 0, 7)
            s = turns(1, 1, 5)
            copy2(1, 0, t, "s")
            copy2(1, 1, s, "v")
            for h in range(3, G):
                mm2(1, acc2[5][:], 5, K[h][5], False, h == G - 1)
            cast2(1, 5, acc2[5][:])
            s = turns(1, 2, 0)
            evac2(1, 5, acc2[5][:], "v")
            copy2(1, 2, s, "s", 0, 64)
            copy2(1, 2, s, "s", 64, P)
            quant_r(1, 0, 256)
            quant_r(1, 256, 384)
            store_words(1, 0, 384)
            quant_r(1, 384, 640)
            quant_r(1, 640, 768)
            store_words(1, 384, 768)
            store_scales(1, nc.scalar)
